import numpy as np, ml_dtypes
CORES = [40,64,80,88,96,104,120,144]
N = 8
import mx_ref
BF = ml_dtypes.bfloat16
def gcols(t, e):
    v = np.concatenate([t.reshape(8, 16, -1, 4), np.zeros((8, 16, 1, 4), BF)], axis=2)
    return np.ascontiguousarray(np.stack([v[g][:, e[g]] for g in range(8)])).reshape(128, -1)
def gpick(z, e):
    return np.concatenate([z[16 * g:16 * g + 16][:, e[g]] for g in range(8)])
def tile(rs):
    return np.stack(rs, axis=2).reshape(128, -1).astype(BF)
def pick(q, e):
    c = np.concatenate([q[0].reshape(128, -1, 4), np.zeros((128, 1, 4), np.uint8)], axis=1); s = np.concatenate([q[1], np.ones((16, 1), np.uint8)], axis=1)
    return (np.ascontiguousarray(c[:, e].reshape(128, -1)), np.ascontiguousarray(s[:, e]))
def join(*qs):
    return (np.concatenate([q[0] for q in qs], axis=1), np.concatenate([q[1] for q in qs], axis=1))
def put(q, e, v):
    c, s = q[0].reshape(128, -1, 4).copy(), q[1].copy(); c[:, e] = v[0].reshape(128, -1, 4); s[:, e] = v[1]
    return (c.reshape(128, -1), s)
def pk(c, s):
    return (np.ascontiguousarray(c), mx_ref.live(s))
def emit(q):
    return q[0], q[1]
def packed(v, rng):
    q = [mx_ref.quantize(np.ascontiguousarray(v[r])) for r in range(N)]
    return np.stack([a for a, b in q]), np.stack([mx_ref.plane(b, rng) for a, b in q])
def values_of_codes():
    e, c = np.zeros((128, 128, 4), np.float32), np.zeros((128, 2, 4), np.uint8)
    e[np.arange(128), np.arange(128), 0] = 1
    c[:127, :, 0] = np.arange(256).reshape(2, 128).T[:127]
    return mx_ref.matmul(mx_ref.quantize(e.reshape(128, 512).astype(BF)), (c.reshape(128, 8), np.full((16, 2), 127, np.uint8))).T.reshape(-1).astype(np.float64)
CODE_VALUE, SCALE_VALUE = values_of_codes(), 2.0 ** (np.arange(256) - 127.0)
def decode(q):
    return (CODE_VALUE[q[0]].reshape(16, 8, -1, 4) * SCALE_VALUE[q[1]][:, None, :, None] + 0.0).reshape(128, -1).astype(np.float32)
def f(rng, *shape):
    return mx_ref.flush((rng.standard_normal(shape, dtype=np.float32) * np.exp2(rng.integers(-2, 3, shape[:-1] + (1,)))).astype(BF))
def wide(rng, *shape, cols=0):
    v = rng.standard_normal(shape, dtype=np.float32) * np.exp2(rng.integers(-12, 13, shape)).astype(np.float32)
    if cols: v *= np.repeat(np.exp2(rng.integers(-cols, cols + 1, shape[:-2] + (1, shape[-1] // 4))) * (rng.random(shape[:-2] + (1, shape[-1] // 4)) > 0.0625), 4, axis=-1).astype(np.float32)
    return mx_ref.flush(v.astype(BF))
C, R = 320, 3
PARTNER = [1, 2, 4]
def fork(m, p):
    base = m + np.maximum(-p[1::16], np.float32(0.0))
    s = p[::16]
    cost = np.stack([base + np.maximum(-s, np.float32(0.0)), base + np.maximum(s, np.float32(0.0))], axis=2).reshape(8, 2 * C) + np.float32(0.0)
    k = np.sort(np.argsort(cost, axis=1, kind="stable")[:, :C], axis=1)
    return k, np.take_along_axis(cost, k, axis=1)
def big(v, k):
    v = v.astype(np.float32) * np.float32(k)
    v[np.abs(v) < np.float32(2.0 ** -16)] = 0
    return v.astype(BF)
def weights(rng, k, still=slice(0)):
    w = big(f(rng, N, 128, 2048), k).reshape(N, 128, 4, 8, 16, 4)
    w[:, :, :, :, still] = 0
    c, p = packed(w.reshape(N, 128, 2048), rng)
    return {"wc": c, "ws": p}
def numbers_of(rng):
    return {"x": big(f(rng, N, 128, 4 * C), 1), "u": np.array(f(rng, N, 128, 512)), "v": np.array(f(rng, N, 128, 512))}
def planted(rng, unit, d, s):
    o = numbers_of(rng)
    x = o["x"].astype(np.float32).reshape(N, 8, 16, C, 4)
    digits = ((d[..., None] >> np.arange(8)) & 1) * 2.0 ** np.arange(8) * unit
    x[:, :, 0] = 0
    x[:, :, 0, :, 0] = -1
    x[:, :, 8] = digits[..., :4]
    x[:, :, 9] = digits[..., 4:]
    x[:, :, 10] = 0
    x[:, :, 10, :, 0] = s
    x[:, :, 11:] = rng.integers(4, 8, (N, 8, 5, C, 4)) * rng.choice([-1.0, 1.0], (N, 8, 5, C, 4)) * (8 * unit)
    u = o["u"].reshape(N, 128, 128, 4)
    u[:, :, ::16] = 0
    u[:, :, 1::16] = 0
    for h in range(0, 128, 16):
        u[:, h + 10, h, 0] = 1
        u[:, h, h + 1, 0] = 1
        u[:, h + 8:h + 10, h + 1] = -1
    return {"x": x.reshape(N, 128, 4 * C).astype(BF), "u": u.reshape(N, 128, 512), "v": o["v"], **weights(rng, 0.25, [0] + [8 + i for i in range(8)])}
def setup_inputs(rng):
    return {**numbers_of(rng), **weights(rng, 1)}
def setup_inputs_ties(rng):
    d = numbers_of(rng)
    e = rng.permutation(N)
    x = d["x"].reshape(N, 8, 16, C, 4)
    for r in range(N):
        k = np.asarray([0, 0, 1, 1, 1, 1, 2])[rng.permutation(C) % 7]
        a = x[r][:, :8, :3].copy()
        a[:, :, 2] = 0
        if r == e[0]: a[:] = 0
        x[r][:, :8] = a[:, :, k]
    x[e[1]] = 0
    u = d["u"].reshape(N, 8, 16, 128, 4)
    u[:, :, 8:, ::16] = 0
    u[:, :, 8:, 1::16] = 0
    g, j = rng.integers(8), rng.integers(C >> R)
    u[e[0], g, :8, 16 * g] = u[e[0], g, :8, 16 * g + 1]
    x[e[0], g, :8, j] = big(u[e[0], g, :8, 16 * g], 1)
    return {"x": x.reshape(N, 128, 4 * C), "u": u.reshape(N, 128, 512), "v": d["v"], **weights(rng, 1, slice(8))}
def setup_inputs_near(rng):
    d = np.argsort(rng.random((N, 8, C)), axis=2) // 2
    q = np.stack([rng.permutation(8) for r in range(N)])
    d[q % 4 == 0] = (np.arange(C) // 2 + C // 4 + 1) % (C // 2)
    o = planted(rng, 2.0 ** -23, d, rng.choice([-1.0, 1.0], (N, 8, C)) * 2.0 ** -23)
    x = o["x"].reshape(N, 8, 16, C, 4)
    for r in range(N):
        for g in range(8):
            if q[r, g] % 2: x[r, g, 0, np.argmax(d[r, g]), 0] = -2.0 ** 30
            if q[r, g] % 4 == 0:
                j = np.argmin(d[r, g])
                x[r, g, :8, j] = 0
                x[r, g, 0, j, 0] = -2.0 ** -24
    return {**o, "x": x.reshape(N, 128, 4 * C)}
def setup_inputs_ends(rng):
    once = np.stack([rng.permutation(8) % 2 for r in range(N)])[:, :, None] == 1
    d = np.where(once, rng.integers(0, 16, (N, 8, C)), (C - 1 - np.arange(C)) // 2)
    s = np.where(once, 4.0, 2.0 ** -9) * rng.choice([-1.0, 1.0], (N, 8, C))
    return planted(rng, 2.0 ** -6, d, s)
def setup_inputs_huge(rng):
    d = numbers_of(rng)
    low = np.where(rng.permutation(N) < N // 2, 0.25, 0.45)[:, None]
    c = low + (0.7 - low) * rng.random((N, C))
    x = 2.0 ** 30 * c[:, None, :, None] * (0.9 + 0.1 * rng.random((N, 128, C, 4)))
    u = d["u"].reshape(N, 128, 128, 4)
    a = 2.0 ** 30 * (1 - 0.25 * rng.random((2, N, 128, 8, 4)))
    u[:, :, ::16] = (a[0] * rng.choice([-1.0, 1.0], a[0].shape)).astype(np.float32).astype(BF)
    u[:, :, 1::16] = (-a[1]).astype(np.float32).astype(BF)
    return {"x": x.astype(np.float32).reshape(N, 128, 4 * C).astype(BF), "u": u.reshape(N, 128, 512), "v": d["v"], **weights(rng, 2.0 ** -8)}
def setup_inputs_spread(rng):
    d = setup_inputs(rng)
    d["x"] = big(wide(rng, N, 128, 4 * C, cols=6), 1)
    return d
def check_inputs(d):
    b = []
    for k in ("x", "u", "v"):
        a = np.abs(d[k].astype(np.float32))
        if not (np.isfinite(a).all() and ((a == 0) | (a >= 2.0 ** -30) & (a <= 2.0 ** 30)).all()): b.append("a value of " + k)
    return b
def reference(x, u, v, wc, ws):
    qu = [mx_ref.quantize(u[r]) for r in range(N)]
    lay = [[pick(pk(wc[r], ws[r]), np.arange(128 * b, 128 * b + 128)) for b in range(4)] for r in range(N)]
    now = [x[r] for r in range(N)]
    m = np.zeros((N, 8, C), np.float32)
    for t in range(R):
        k, z, sent = [], [], []
        for r in range(N):
            q = mx_ref.quantize(now[r])
            e, m[r] = fork(m[r], mx_ref.matmul(qu[r], q))
            k.append(e)
            z.append(gcols(decode(q).astype(BF), e // 2))
            sent.append(mx_ref.quantize(z[r]))
        for r in range(N):
            sign = np.repeat(1 - 2 * (k[r] % 2), 16, axis=0).astype(np.float32)
            h = [gpick(mx_ref.matmul(lay[r][b], sent[r ^ PARTNER[t]]) * np.float32(0.015625), k[r] // 2) for b in range(4)]
            a = z[r].astype(np.float32).reshape(128, C, 4)
            now[r] = tile([a[:, :, b] + sign * h[b] for b in range(4)])
    y, kl = np.zeros((N, 128, C), np.float32), np.zeros((N, 8, C), np.float32)
    oc, osc = np.zeros((N, 128, 4 * C), np.uint8), np.zeros((N, 16, C), np.uint8)
    for r in range(N):
        q = mx_ref.quantize(now[r])
        y[r] = mx_ref.matmul(mx_ref.quantize(v[r]), q)
        kl[r] = k[r]
        oc[r], osc[r] = emit(q)
    return {"y": y, "kl": kl, "ml": m, "oc": oc, "osc": osc}

@@ -1,0 +1,439 @@
+from concourse.bass import DstId, RemoteDMATransfer
+from concourse.mybir import dt, AluOpType, ActivationFunctionType
+
+C = 320
+F = 2 * C
+ROUNDS = 3
+PARTNER = [1, 2, 4]
+TAU = 2.0 ** -100
+SL = 36
+GW = 192
+SHARE = {3: 112, 5: 160, 7: 192, 8: 192}
+Q4 = "float8_e4m3fn_x4"
+
+SCRATCH = {}
+for _dt, _list in (
+    ("bfloat16", (("xt", 4 * C), ("tt", 4 * C), ("ut", 512), ("vt", 512), ("eb", 1040), ("zt", 4 * C), ("dp", 4 * C), ("dn", 2 * C),
+                  ("tw", 4 * F), ("junk", F), ("slt", F + 2), ("nle", F + 2), ("onm", F + 2), ("yy", F + 2), ("kk", F + 2),
+                  ("dmp", C), ("dmn", C), ("ga", C), ("gb", C), ("jv", C), ("fi", C), ("gf", C),
+                  ("gl", GW + 32), ("md", GW + 32), ("mo", GW + 32), ("sw0", 976), ("sw1", 976), ("sw2", 976))),
+    ("float32", (("pf", 8), ("jf", C), ("f1", 16), ("f2", 16), ("t1", 16), ("t2", 16), ("z16", 16), ("mk0", 32), ("mk", 32), ("mk2", 32),
+                 ("d12", 2 * SL), ("co", 6 * SL), ("dd", 6 * SL), ("fl", 32), ("ft", SL), ("rr", 8 * SL), ("sc", 16),
+                 ("nz", C), ("ab", C), ("r0", C), ("r1", C), ("xx", F), ("ci", F), ("dv", F), ("mm", C),
+                 ("e1", 20), ("e2", 20), ("e3", 20), ("cw", 20), ("jc", C), ("c2", C), ("xw", C), ("k2", C), ("gk", C), ("kf", C), ("yo", C))),
+    ("int32", (("pi", 8), ("ui", 16), ("ai", C), ("a2", C))),
+    ("uint16", (("uo", 16), ("so", 20), ("ko", 20), ("ao0", 20), ("ao1", 20), ("ao2", 20), ("la0", 20), ("la1", 20), ("la2", 20))),
+    (Q4, (("uq", 128), ("uq2", 256), ("vq", 128), ("wq", 512), ("eq", 768), ("zq", C),
+          ("tq0", C), ("tq1", C), ("tq2", C), ("tq3", C), ("pq0", C), ("pq1", C), ("pq2", C))),
+    ("uint8", (("us", 128), ("us2", 256), ("vs", 128), ("wp", 512), ("es", 768), ("zs", C),
+               ("ts0", C), ("ts1", C), ("ts2", C), ("ts3", C), ("ps0", C), ("ps1", C), ("ps2", C))),
+):
+    for _name, _n in _list:
+        SCRATCH[_name] = ("sbuf", [128, _n], _dt)
+for _b in range(8):
+    SCRATCH["bk%d" % _b] = ("psum", [128, 512], "float32")
+
+SEMAPHORES = (["sv", "sa", "sp", "sg", "sent", "ldu", "ldx", "ldv", "ldw", "stk", "sto", "sty"]
+              + ["bulk%d" % t for t in range(ROUNDS)] + ["lst%d" % t for t in range(ROUNDS)])
+
+A = AluOpType
+AF = ActivationFunctionType
+
+
+def bits(engines):
+    m = 0
+    for e in engines:
+        m |= 1 << e
+    return m
+
+
+def helpers(me, other, topo):
+    ok = [c for c in topo.cores_of(me) if c != me and topo.may_write(c, other)]
+    near = [c for c in ok if topo.die(c) == topo.die(me)]
+    far = [c for c in ok if topo.die(c) != topo.die(me)]
+    return near[0], near[1], far[0]
+
+
+def helper_program(g, core, T, topo):
+    sent = 0
+    H = C // 2
+    for t in range(ROUNDS):
+        for r, me in enumerate(T.cores):
+            other = T.cores[r ^ PARTNER[t]]
+            h1, h2, h3 = helpers(me, other, topo)
+            if core not in (h1, h2, h3):
+                continue
+            rid, pid = topo.addr(other, core)
+            mask = topo.mask(core, other)
+            n_out = len(topo.engines(core, other))
+            n_in = len(topo.engines(me, core))
+            bulk, lst = T.sem["bulk%d" % t], T.sem["lst%d" % t]
+            if core == h2:
+                g.wait_ge(bulk, n_in)
+                v = T["ps%d" % t][:]
+                g.remote_dma(v, v, bulk, T.sem.sent, pid, rid, mask)
+                g.wait_ge(lst, n_in)
+                v = T["la%d" % t][:]
+                g.remote_dma(v, v, lst, T.sem.sent, pid, rid, mask)
+                sent += 2 * n_out
+            else:
+                a = 0 if core == h1 else H
+                g.wait_ge(bulk, n_in // 2)
+                g.remote_dma(T["pq%d" % t][:, a:a + H].bitcast(dt.uint8), T["pq%d" % t][:, a:a + H].bitcast(dt.uint8),
+                             bulk, T.sem.sent, pid, rid, mask)
+                sent += n_out
+    if sent:
+        g.wait_ge(T.sem.sent, sent)
+
+
+def rank_program(g, core, T, topo):
+    rank = T.rank_of(core)
+    if rank is None:
+        helper_program(g, core, T, topo)
+        return
+
+    V, S, P, Y = g.vector, g.scalar, g.tensor, g.sync
+    queue = {"v": V, "a": S, "p": P, "g": g, "y": Y}
+    own = {"v": "sv", "a": "sa", "p": "sp", "g": "sg"}
+    count = {}
+    known = {e: {} for e in queue}
+    writer, readers = {}, {}
+
+    def need(e, ev):
+        sem, val, clock = ev
+        if e == "p" and sem == "sp":
+            return
+        if known[e].get(sem, 0) < val:
+            queue[e].wait_ge(T.sem[sem], val)
+            known[e][sem] = val
+        for s, n in clock.items():
+            if known[e].get(s, 0) < n:
+                known[e][s] = n
+
+    def op(e, call, reads, writes, sem=None, step=1, total=None):
+        evs = [writer[k] for k in reads if k in writer]
+        for k in writes:
+            if k in writer:
+                evs.append(writer[k])
+            evs += readers.get(k, [])
+        top = {}
+        for ev in evs:
+            if ev[0] not in top or top[ev[0]][1] < ev[1]:
+                top[ev[0]] = ev
+        evs = list(top.values())
+        for ev in evs:
+            if not any(o is not ev and o[2].get(ev[0], 0) >= ev[1] for o in evs):
+                need(e, ev)
+        ins = call()
+        if step == 0:
+            return
+        s = sem or own[e]
+        ins.then_inc(T.sem[s], step)
+        count[s] = count.get(s, 0) + step
+        ev = (s, total or count[s], dict(known[e]))
+        for k in reads:
+            readers.setdefault(k, []).append(ev)
+        for k in writes:
+            writer[k] = ev
+            readers[k] = []
+
+    def ts(out, in0, s1, s2, o0, o1, reads, writes):
+        if o1 is None:
+            op("v", lambda: V.tensor_scalar(out, in0, s1, None, o0), reads, writes)
+        else:
+            op("v", lambda: V.tensor_scalar(out, in0, s1, s2, o0, o1), reads, writes)
+
+    def tt(out, in0, in1, o, reads, writes):
+        op("v", lambda: V.tensor_tensor(out, in0, in1, o), reads, writes)
+
+    def scan(out, d0, d1, init, o0, o1, reads, writes):
+        op("v", lambda: V.tensor_tensor_scan(out, d0, d1, init, o0, o1), reads, writes)
+
+    def fill(ap, val, writes):
+        op("v", lambda: V.memset(ap, val), [], writes)
+
+    def cp(out, in_, reads, writes):
+        op("v", lambda: V.tensor_copy(out, in_), reads, writes)
+
+    def act(out, in_, f, reads, writes, **kw):
+        op("a", lambda: S.activation(out, in_, f, **kw), reads, writes)
+
+    def quant(q, s, t, reads, writes):
+        op("v", lambda: V.quantize_mx(q, s, t), reads, writes)
+
+    def mx(bank, lq, ls, rq, rs, start, stop, reads):
+        op("p", lambda: P.matmul_mx(T["bk%d" % bank][:, 0:C], lq, ls, rq, rs, start, stop), reads, ["bk%d" % bank])
+
+    def bank(b):
+        return T["bk%d" % b][:, 0:C]
+
+    def unit(bk, e, q, s, stop, reads):
+        mx(bk, T.eq[:, 128 * e:128 * e + 128], T.es[:, 128 * e:128 * e + 128], q[:], s[:], True, stop, ["eq%d" % e] + reads)
+
+    op("y", lambda: Y.dma_start(T.ut[:], T.u[:]), [], ["ut"], sem="ldu", step=16)
+    op("a", lambda: S.dma_start(T.xt[:], T.x[:]), [], ["xt"], sem="ldx", step=16)
+
+    op("g", lambda: g.iota(T.pi[:, 0:1], [[0, 1]], 0, 1), [], ["pi0"])
+    op("g", lambda: g.iota(T.ui[:], [[-1, 2], [16, 8]], 1, 0), [], ["ui"])
+    op("g", lambda: g.iota(T.jf[:], [[1, C]], C, 0, allow_small_or_imprecise_dtypes=True), [], ["jf"])
+    op("g", lambda: g.iota(T.ai[:], [[1, C]], 256, -1), [], ["ai"])
+
+    fill(T.co[:], 0.0, ["co"])
+    fill(T.d12[:], 1.0, ["d12"])
+    fill(T.z16[:], 0.0, ["z16"])
+    fill(T.ft[:], 0.0, ["ft"])
+    ts(T.pi[:, 1:2], T.pi[:, 0:1], 15, None, A.bitwise_and, None, ["pi0"], ["pi1"])
+    ts(T.pi[:, 2:3], T.pi[:, 0:1], 4, 1, A.logical_shift_right, A.bitwise_and, ["pi0"], ["pi2"])
+    cp(T.uo[:], T.ui[:], ["ui"], ["uo"])
+    R1, R320, HH = T.pf[:, 0:1], T.pf[:, 1:2], T.pf[:, 2:3]
+    ts(R1, T.pi[:, 1:2], 1.0, None, A.add, None, ["pi1"], ["R1"])
+    ts(R320, T.pi[:, 1:2], float(C), None, A.add, None, ["pi1"], ["R320"])
+    cp(HH, T.pi[:, 2:3], ["pi2"], ["HH"])
+    fill(T.co[:, 4 * SL + 33:4 * SL + 34], -2.0 ** -25, ["co"])
+    fill(T.co[:, 5 * SL + 32:5 * SL + 33], 2.0 ** -25, ["co"])
+    ts(T.f2[:], T.jf[:, 0:16], R320, 1.0, A.is_le, A.add, ["jf", "R320"], ["f2"])
+    ts(T.mk0[:], T.jf[:, 0:32], float(C + 16), HH, A.is_ge, A.not_equal, ["jf", "HH"], ["mk0"])
+    ts(T.f1[:], T.f2[:], 4095.0, -4094.0, A.mult, A.add, ["f2"], ["f1"])
+    scan(T.t2[:], T.f2[:], T.z16[:], 1.0, A.mult, A.add, ["f2", "z16"], ["t2"])
+    ts(T.mk[:], T.mk0[:], -1024.0, None, A.mult, None, ["mk0"], ["mk"])
+    scan(T.t1[:], T.f1[:], T.z16[:], TAU, A.mult, A.add, ["f1", "z16"], ["t1"])
+
+    act(T.d12[:, SL + 32:SL + 33], R1, AF.Identity, ["R1"], ["d12"], scale=1.0 / 16, bias=1.0)
+    for k in range(4):
+        act(T.co[:, k * SL + 32:k * SL + 33], R1, AF.Identity, ["R1", "co"], ["co%d" % k], scale=2.0 ** (-8 - 4 * k))
+    act(T.co[:, 4 * SL + 34:4 * SL + 35], R1, AF.Identity, ["R1", "co"], ["co4"], scale=2.0 ** -23)
+    act(T.d12[:, 32:33], T.t2[:, 15:16], AF.Identity, ["t2"], ["d12"])
+
+    quant(T.uq[:], T.us[:], T.ut[:], ["ut"], ["uq"])
+    cp(T.uq2[:].bitcast(dt.uint32), T.uq[:].bitcast(dt.uint32).indirect(T.uo[:]), ["uq", "uo"], ["uq2"])
+    act(T.us2[:], T.us[:].indirect(T.uo[:]), AF.Copy, ["uq", "uo"], ["us2"])
+
+    def extras(k):
+        if k == 0:
+            fill(T.eb[:], 0.0, ["eb"])
+            fill(T.onm[:, 2:F + 2], -1.0, ["onm"])
+        if k == 2:
+            act(T.jv[:], T.jf[:], AF.Identity, ["jf"], ["jv"], bias=-480.0)
+        if k == 3:
+            act(T.jc[:], T.jf[:], AF.Identity, ["jf"], ["jc"], scale=4.0, bias=-1598.0)
+            ts(T.eb[:, 3:515:4], T.ai[:, 0:128], 256.0, 64.0, A.is_equal, A.mult, ["ai", "eb"], ["e+"])
+            ts(T.eb[:, 523:1035:4], T.ai[:, 0:128], 256.0, -64.0, A.is_equal, A.mult, ["ai", "eb"], ["e-"])
+            fill(T.onm[:, 0:1], float(C), ["onm0"])
+            fill(T.onm[:, 1:2], 0.0, ["onm1"])
+        if k == 4:
+            act(T.c2[:], T.jf[:], AF.Identity, ["jf"], ["c2"], scale=2.0, bias=-640.0)
+        if k == 5:
+            for b in range(4):
+                quant(T.eq[:, 128 * b:128 * b + 128], T.es[:, 128 * b:128 * b + 128], T.eb[:, 3 - b:515 - b], ["e+"], ["eq%d" % b])
+            op("y", lambda: Y.dma_start(T.vt[:], T.v[:]), ["eq3"], ["vt"], sem="ldv", step=16)
+            op("y", lambda: Y.dma_start(T.wq[:].bitcast(dt.uint8), T.wc[:]), [], ["wq"], sem="ldw", step=16, total=32)
+            op("y", lambda: Y.dma_start(T.wp[:], T.ws[:]), [], ["wp"], sem="ldw", step=16, total=32)
+        if k == 7:
+            ts(T.a2[:], T.ai[:], 15, None, A.bitwise_and, None, ["ai"], ["a2"])
+            fill(T.sw0[:, 0:C], -256.0, ["sw0"])
+            ts(T.cw[:], T.jf[:, 0:C:16], R1, 2.0, A.add, A.mult, ["jf", "R1"], ["cw"])
+            fill(T.slt[:, 0:2], 0.0, ["sltp"])
+        if k == 8:
+            ts(T.dmp[:], T.a2[:], 0.0, 2048.0, A.is_equal, A.mult, ["a2"], ["dmp"])
+            fill(T.nle[:, 0:2], 0.0, ["nlep"])
+            ts(T.dmn[:], T.dmp[:], -1.0, None, A.mult, None, ["dmp"], ["dmn"])
+        if k == 9:
+            for b in (2, 3):
+                quant(T.eq[:, 256 + 128 * b:384 + 128 * b], T.es[:, 256 + 128 * b:384 + 128 * b], T.eb[:, 523 - b:1035 - b], ["e-"], ["eq%d" % (2 + b)])
+        if k == 10:
+            fill(T.md[:, 0:GW], -1.0, ["md0"])
+            fill(T.gl[:, GW:GW + 32], 0.0, ["glt"])
+            cp(T.md[:, GW:GW + 1], T.mk[:, 0:1], ["mk"], ["md1"])
+            tt(T.md[:, GW + 1:GW + 32], T.mk[:, 1:32], T.mk[:, 0:31], A.subtract, ["mk"], ["md2"])
+
+    def lo(k):
+        return T.rr[:, (k - 1) * SL + 31:(k - 1) * SL + 32]
+
+    sent = 0
+    H = C // 2
+    for t in range(ROUNDS):
+        other = T.cores[rank ^ PARTNER[t]]
+        h1, h2, h3 = helpers(core, other, topo)
+        tq, tsc, pq, psc = T["tq%d" % t], T["ts%d" % t], T["pq%d" % t], T["ps%d" % t]
+        ao, la, sw = T["ao%d" % t], T["la%d" % t], T["sw%d" % t]
+        ktq, kao, ksw = "tq%d" % t, "ao%d" % t, "sw%d" % t
+        bulk, lst = T.sem["bulk%d" % t], T.sem["lst%d" % t]
+        if t == 0:
+            quant(tq[:], tsc[:], T.xt[:], ["xt"], [ktq])
+            extras(0)
+        else:
+            quant(tq[:], tsc[:], T.tt[:], ["tt0", "tt1", "tt2", "tt3"], [ktq])
+
+        eng = topo.engines(core, h1)
+        n = len(eng)
+        trs = []
+        for h, a, es in ((h1, 0, eng[:n // 2]), (h3, H, eng[n // 2:])):
+            rid, pid = topo.addr(h, core)
+            trs.append(RemoteDMATransfer(dst_ids=[DstId(rid=rid, pnc=pid)], dma_engine_mask=bits(es), remote_sem=bulk,
+                                         src=tq[:, a:a + H].bitcast(dt.uint8), dst=pq[:, a:a + H].bitcast(dt.uint8)))
+        rid2, pid2 = topo.addr(h2, core)
+        op("g", lambda: g.remote_dma_fused(trs, local_sem=T.sem.sent), [ktq], [], step=0)
+        op("g", lambda: g.remote_dma(psc[:], tsc[:], bulk, T.sem.sent, pid2, rid2, bits(eng)), [ktq], [], step=0)
+        sent += 3 * n
+        oh = helpers(other, core, topo)
+        writer["pq"] = ("bulk%d" % t, sum(len(topo.engines(h, core)) for h in oh), {})
+        readers["pq"] = []
+        writer["la"] = ("lst%d" % t, len(topo.engines(oh[1], core)), {})
+        readers["la"] = []
+
+        mx(0, T.uq2[:, 0:128], T.us2[:, 0:128], tq[:], tsc[:], True, True, ["uq2", "us2", ktq])
+        mx(1, T.uq2[:, 128:256], T.us2[:, 128:256], tq[:], tsc[:], True, True, ["uq2", "us2", ktq])
+        B, HI = T.xx[:, 0:C], T.xx[:, C:F]
+        t1 = T.t1[:, 15:16]
+        if t == 0:
+            act(B, bank(0), AF.Relu, ["bk0"], ["B"], scale=-1.0)
+        else:
+            act(T.nz[:], bank(0), AF.Relu, ["bk0"], ["nz"], scale=-1.0)
+            tt(B, T.mm[:], T.nz[:], A.add, ["mm", "nz"], ["B"])
+        act(T.ab[:], bank(1), AF.Abs, ["bk1"], ["ab"])
+        tt(HI, B, T.ab[:], A.add, ["B", "ab"], ["HI"])
+        if t > 0:
+            act(T.r0[:], bank(1), AF.Relu, ["bk1"], ["r0"], scale=-1.0)
+        act(T.junk[:, 0:C], B, AF.Sign, ["B", "t1"], ["j0", "s0"], scale=-1.0, bias=t1, accum_out=T.sc[:, 0:1])
+        if t == 0:
+            act(T.r0[:], bank(1), AF.Relu, ["bk1"], ["r0"], scale=-1.0)
+        ts(T.mk2[:], T.mk[:], T.sc[:, 0:1], None, A.subtract, None, ["mk", "s0"], ["mk2"])
+
+        thr, kthr = t1, "t1"
+        for k in range(1, 9):
+            sk = T.sc[:, k:k + 1]
+            d = SHARE.get(k, 0) if t > 0 else 0
+            src, ksrc = (T.xx, ["B", "HI"]) if k < 8 else (T.dv, ["dv"])
+            if k == 1:
+                act(T.junk[:, C:F], HI, AF.Sign, ["HI", kthr], ["j1", "s1"], scale=-1.0, bias=thr, accum_out=sk)
+                act(T.r1[:], bank(1), AF.Relu, ["bk1"], ["r1"])
+            else:
+                act(T.junk[:, d:F], src[:, d:F], AF.Sign, ksrc + [kthr], ["j0", "j1", "s%d" % k], scale=-1.0, bias=thr, accum_out=sk)
+            if d:
+                ts(T.gl[:, GW - d:GW], src[:, 0:d], thr, 2.0, A.is_gt, A.mult, ksrc + [kthr], ["gl"])
+            if k == 2:
+                tt(T.ci[:, 0:F:2], B, T.r0[:], A.add, ["B", "r0"], ["c0"])
+            if k == 3:
+                ts(T.dd[:], T.co[:], lo(2), None, A.mult, None, ["co", "co0", "co1", "co2", "co3", "co4", "rr2"], ["dd", "nb"])
+            if k == 4:
+                tt(T.ci[:, 1:F:2], B, T.r1[:], A.add, ["B", "r1"], ["c1"])
+            nb = T.dd[:, 4 * SL + 32:4 * SL + 33]
+            if k == 5:
+                ts(nb, lo(2), 2.0 ** -8, lo(3), A.mult, A.subtract, ["rr2", "rr3"], ["nb"])
+            if k == 6:
+                ts(T.dv[:], T.ci[:], TAU, nb, A.max, A.add, ["c0", "c1", "nb"], ["dv"])
+            if t == 0:
+                extras(k)
+            if d:
+                scan(T.mo[:, GW - d:GW + 32], T.gl[:, GW - d:GW + 32], T.md[:, GW - d:GW + 32], 0.0, A.add, A.add,
+                     ["gl", "glt", "md0", "md1", "md2"], ["mo"])
+                mask, kmask = T.mo[:, GW:GW + 32], "mo"
+            elif k == 1:
+                mask, kmask = T.mk2[:], "mk2"
+            else:
+                mask, kmask = T.mk[:], "mk"
+            ts(T.fl[:], mask, sk, thr, A.is_gt, A.mult, [kmask, "s%d" % k, kthr], ["fl"])
+            op("v", lambda: V.transpose(T.ft[:, 0:32], T.fl[:]), ["fl"], ["ft"])
+            w = 35 if k == 7 else 33
+            if k <= 2:
+                d1, o1, kd = T.d12[:, (k - 1) * SL:(k - 1) * SL + w], A.mult, ["d12"]
+            else:
+                d1, o1, kd = T.dd[:, (k - 3) * SL:(k - 3) * SL + w], A.add, ["dd"] + (["nb"] if k == 7 else [])
+            if k == 1:
+                init, ki = TAU, []
+            elif k == 8:
+                init, ki = T.rr[:, 6 * SL + 33:6 * SL + 34], ["rr7"]
+            else:
+                init, ki = lo(k - 1), ["rr%d" % (k - 1)]
+            o = (k - 1) * SL
+            scan(T.rr[:, o:o + w], T.ft[:, 0:w], d1, init, A.max, o1, ["ft"] + kd + ki, ["rr%d" % k])
+            thr, kthr = T.rr[:, o + w - 1:o + w], "rr%d" % k
+
+        act(T.slt[:, 2:F + 2], T.dv[:], AF.Sign, ["dv", "rr8"], ["slt", "s9"], scale=-1.0, bias=lo(8), accum_out=T.sc[:, 9:10])
+        ts(T.nle[:, 2:F + 2], T.dv[:], thr, -2.0, A.is_le, A.mult, ["dv", "rr8"], ["nle"])
+        scan(T.yy[:], T.onm[:], T.slt[:], T.sc[:, 9:10], A.add, A.subtract, ["onm", "onm0", "onm1", "slt", "sltp", "s9"], ["yy"])
+        scan(T.kk[:], T.nle[:], T.yy[:], float(C), A.add, A.max, ["nle", "nlep", "yy"], ["kk"])
+        scan(T.ga[:], T.dmn[:], T.kk[:, 1:F + 1:2], 0.0, A.add, A.max, ["dmn", "kk"], ["ga"])
+        scan(T.gb[:], T.dmn[:], T.kk[:, 3:F + 2:2], 0.0, A.add, A.max, ["dmn", "kk"], ["gb"])
+        tt(T.e1[:], T.ga[:, 15:C:16], T.gb[:, 15:C:16], A.is_equal, ["ga", "gb"], ["e1"])
+        tt(T.e2[:], T.e1[:], T.cw[:], A.mult, ["e1", "cw"], ["e2"])
+        tt(T.e3[:], T.e2[:], T.ga[:, 15:C:16], A.subtract, ["e2", "ga"], ["e3"])
+        ts(T.so[:], T.e3[:], float(C), 0.5, A.add, A.mult, ["e3"], ["so"])
+        cp(sw[:, 0:976].indirect(T.so[:]), T.jv[:], ["so", "jv"], [ksw])
+        scan(T.fi[:], sw[:, 0:C], sw[:, 0:C], -256.0, A.max, A.max, [ksw], ["fi"])
+        scan(T.gf[:], T.dmp[:], T.fi[:], 0.0, A.add, A.min, ["dmp", "fi"], ["gf"])
+        ts(ao[:], T.gf[:, 15:C:16], float(H), None, A.add, None, ["gf"], [kao])
+        op("g", lambda: g.remote_dma(la[:], ao[:], lst, T.sem.sent, pid2, rid2, bits(eng)), [kao], [], step=0)
+
+        for b in (0, 1):
+            unit(2 + b, b, tq, tsc, True, [ktq])
+        for b in range(4):
+            unit(4 + b, b, pq, psc, True, ["pq"])
+        for b in (0, 1):
+            act(T.dn[:, C * b:C * b + C], bank(2 + b), AF.Copy, ["bk%d" % (2 + b)], ["dn%d" % b])
+        for b in range(4):
+            act(T.dp[:, C * b:C * b + C], bank(4 + b), AF.Identity, ["bk%d" % (4 + b)], ["dp%d" % b], scale=1.0 / 64)
+
+        tt(T.xw[:], T.kk[:, 2:F + 2:2], T.jc[:], A.add, ["kk", "jc"], ["xw"])
+        if t == 0:
+            extras(9)
+        tt(T.k2[:], T.xw[:].indirect(ao[:]), T.c2[:], A.add, ["xw", kao, "c2"], ["k2"])
+        scan(T.gk[:], T.dmp[:], T.k2[:], 0.0, A.add, A.min, ["dmp", "k2"], ["gk"])
+        if t + 1 < ROUNDS:
+            fill(T["sw%d" % (t + 1)][:, 0:C], -256.0, ["sw%d" % (t + 1)])
+        ts(T.ko[:], T.gk[:, 15:C:16], 0.5, None, A.mult, None, ["gk"], ["ko"])
+        act(T.mm[:], T.ci[:].indirect(T.ko[:]), AF.Copy, ["c0", "c1", "ko"], ["mm"])
+        if t == 0:
+            extras(10)
+        if t == 1:
+            quant(T.vq[:], T.vs[:], T.vt[:], ["vt"], ["vq"])
+        if t == ROUNDS - 1:
+            ts(T.kf[:], T.k2[:], 0.5, None, A.mult, None, ["k2"], ["kf"])
+            op("y", lambda: Y.dma_start(T.kl[:], T.kf[0:128:16, :]), ["kf"], [], sem="stk", step=16)
+            op("y", lambda: Y.dma_start(T.ml[:], T.mm[0:128:16, :]), ["mm"], [], sem="stk", step=16)
+        for b in (2, 3):
+            unit(2 * b, b, tq, tsc, False, [ktq])
+            unit(2 * b + 1, 2 + b, tq, tsc, False, [ktq])
+
+        for b in (0, 1):
+            cp(T.zt[:, b:4 * C:4], T.dp[:, C * b:C * b + C].indirect(la[:]), ["dp%d" % b, "la"], ["zt%d" % b])
+        for b in (2, 3):
+            act(T.zt[:, b:4 * C:4], T.dp[:, C * b:C * b + C].indirect(la[:]), AF.Copy, ["dp%d" % b, "la"], ["zt%d" % b])
+        quant(T.zq[:], T.zs[:], T.zt[:], ["zt0", "zt1", "zt2", "zt3"], ["zq"])
+        for b, bk in ((0, 0), (2, 4), (2, 5), (1, 1), (3, 6), (3, 7)):
+            mx(bk, T.wq[:, 128 * b:128 * b + 128], T.wp[:, 128 * b:128 * b + 128], T.zq[:], T.zs[:], b < 2, True, ["wq", "wp", "zq"])
+
+        def child(b, s):
+            out, wr = T.tw[:, F * b + s:F * b + F:2], ["tw%d%d" % (b, s)]
+            if b < 2:
+                tt(out, T.dn[:, C * b:C * b + C], bank(b), A.add if s == 0 else A.subtract, ["dn%d" % b, "bk%d" % b], wr)
+            else:
+                act(out, bank(2 * b + s), AF.Identity, ["bk%d" % (2 * b + s)], wr, scale=2.0 ** -6 if s == 0 else -2.0 ** -6)
+
+        def pick(b):
+            out, win = T.tt[:, b:4 * C:4], T.tw[:, F * b:F * b + F].indirect(T.ko[:])
+            rd, wr = ["tw%d0" % b, "tw%d1" % b, "ko"], ["tt%d" % b]
+            if b < 2:
+                ts(out, win, 2.0 ** -6, None, A.mult, None, rd, wr)
+            else:
+                act(out, win, AF.Copy, rd, wr)
+
+        for b in (0, 2):
+            child(b, 0)
+            child(b, 1)
+            child(b + 1, 0)
+            pick(b)
+            child(b + 1, 1)
+            pick(b + 1)
+
+    tq, tsc, ktq = T["tq%d" % ROUNDS], T["ts%d" % ROUNDS], "tq%d" % ROUNDS
+    quant(tq[:], tsc[:], T.tt[:], ["tt0", "tt1", "tt2", "tt3"], [ktq])
+    mx(0, T.vq[:], T.vs[:], tq[:], tsc[:], True, True, ["vq", ktq])
+    op("y", lambda: Y.dma_start(T.oc[:], tq[:].bitcast(dt.uint8)), [ktq], [], sem="sto", step=16)
+    for k in range(4):
+        op("y", lambda: Y.dma_start(T.osc[4 * k:4 * k + 4, :], tsc[32 * k:32 * k + 4, :]), [ktq], [], sem="sto", step=16)
+    act(T.yo[:], bank(0), AF.Copy, ["bk0"], ["yo"])
+    op("a", lambda: S.dma_start(T.y[:], T.yo[:]), ["yo"], [], sem="sty", step=16)
+    g.wait_ge(T.sem.sent, sent)
+    for s in ("sg", "sv", "sp", "sa", "stk", "sto", "sty"):
+        g.wait_ge(T.sem[s], count[s])

@@ -8,20 +8,29 @@ PARTNER = [1, 2, 4]
 TAU = 2.0 ** -100
 SL = 36
 GW = 192
-SHARE = {3: 112, 5: 160, 7: 192, 8: 192}
+SHARE = {1: 64, 2: 192, 3: 144, 4: 192, 5: 112, 6: 112, 7: 144, 8: 192}
+SHARE0 = {5: 112, 6: 112, 7: 144, 8: 144}
+CP = C // 16
+FP = 2 * CP
+PW = 32 + 1 + FP
+PE = 76
+PL = 512
+SW = PL + 3 * C
 Q4 = "float8_e4m3fn_x4"
 
 SCRATCH = {}
 for _dt, _list in (
     ("bfloat16", (("xt", 4 * C), ("tt", 4 * C), ("ut", 512), ("vt", 512), ("eb", 1040), ("zt", 4 * C), ("dp", 4 * C), ("dn", 2 * C),
-                  ("tw", 4 * F), ("junk", F), ("slt", F + 2), ("nle", F + 2), ("onm", F + 2), ("yy", F + 2), ("kk", F + 2),
-                  ("dmp", C), ("dmn", C), ("ga", C), ("gb", C), ("jv", C), ("fi", C), ("gf", C),
-                  ("gl", GW + 32), ("md", GW + 32), ("mo", GW + 32), ("sw0", 976), ("sw1", 976), ("sw2", 976))),
-    ("float32", (("pf", 8), ("jf", C), ("f1", 16), ("f2", 16), ("t1", 16), ("t2", 16), ("z16", 16), ("mk0", 32), ("mk", 32), ("mk2", 32),
+                  ("tw", 4 * F), ("junk", F), ("jk2", 2 * FP), ("dmp", C), ("jv", C), ("jm", C), ("fi", C), ("gf", C), ("bt", C),
+                  ("gl", GW + 32), ("md", GW + 32), ("mo", GW + 32), ("sw0", SW), ("sw1", SW), ("sw2", SW))),
+    ("float32", (("pf", 8), ("jf", 32), ("f1", 16), ("f2", 16), ("t1", 16), ("t2", 16), ("z16", 16), ("mk0", 32), ("mk", 32), ("mk2", 32),
                  ("d12", 2 * SL), ("co", 6 * SL), ("dd", 6 * SL), ("fl", 32), ("ft", SL), ("rr", 8 * SL), ("sc", 16),
-                 ("nz", C), ("ab", C), ("r0", C), ("r1", C), ("xx", F), ("ci", F), ("dv", F), ("mm", C),
-                 ("e1", 20), ("e2", 20), ("e3", 20), ("cw", 20), ("jc", C), ("c2", C), ("xw", C), ("k2", C), ("gk", C), ("kf", C), ("yo", C))),
-    ("int32", (("pi", 8), ("ui", 16), ("ai", C), ("a2", C))),
+                 ("nz", C), ("ab", C), ("rv", F), ("xx", F), ("dv", F), ("mm", C), ("bg", C), ("mo1", GW + 32),
+                 ("bd", CP), ("rd", FP), ("cd", FP), ("dvd", FP), ("fg", 2 * PE), ("cs", PE), ("ke", PE), ("kt", PE), ("kk", 44),
+                 ("sm", 32), ("tg", 32), ("me", 32), ("ml2", 32), ("fl2", 64),
+                 ("ha", 3 * CP), ("hb", 3 * CP), ("hs", 3 * CP),
+                 ("kh", C), ("gk", C), ("kf", C), ("yo", C))),
+    ("int32", (("pi", 8), ("ui", 16), ("ai", 128))),
     ("uint16", (("uo", 16), ("so", 20), ("ko", 20), ("ao0", 20), ("ao1", 20), ("ao2", 20), ("la0", 20), ("la1", 20), ("la2", 20))),
     (Q4, (("uq", 128), ("uq2", 256), ("vq", 128), ("wq", 512), ("eq", 768), ("zq", C),
           ("tq0", C), ("tq1", C), ("tq2", C), ("tq3", C), ("pq0", C), ("pq1", C), ("pq2", C))),
@@ -33,7 +42,7 @@ for _dt, _list in (
 for _b in range(8):
     SCRATCH["bk%d" % _b] = ("psum", [128, 512], "float32")
 
-SEMAPHORES = (["sv", "sa", "sp", "sg", "sent", "ldu", "ldx", "ldv", "ldw", "stk", "sto", "sty"]
+SEMAPHORES = (["sv", "sa", "sp", "sg", "sent", "ldu", "ldx", "ldv", "ldw", "stk", "sto", "sty", "deal"]
               + ["bulk%d" % t for t in range(ROUNDS)] + ["lst%d" % t for t in range(ROUNDS)])
 
 A = AluOpType
@@ -170,81 +179,94 @@ def rank_program(g, core, T, topo):
     def unit(bk, e, q, s, stop, reads):
         mx(bk, T.eq[:, 128 * e:128 * e + 128], T.es[:, 128 * e:128 * e + 128], q[:], s[:], True, stop, ["eq%d" % e] + reads)
 
+    def clear(t):
+        fill(T["sw%d" % t][:, 0:C], -256.0, ["swa%d" % t])
+        fill(T["sw%d" % t][:, PL:PL + C], -256.0, ["swb%d" % t])
+
     op("y", lambda: Y.dma_start(T.ut[:], T.u[:]), [], ["ut"], sem="ldu", step=16)
     op("a", lambda: S.dma_start(T.xt[:], T.x[:]), [], ["xt"], sem="ldx", step=16)
 
     op("g", lambda: g.iota(T.pi[:, 0:1], [[0, 1]], 0, 1), [], ["pi0"])
+    op("g", lambda: g.iota(T.jf[:], [[1, 32]], C, 0, allow_small_or_imprecise_dtypes=True), [], ["jf"])
     op("g", lambda: g.iota(T.ui[:], [[-1, 2], [16, 8]], 1, 0), [], ["ui"])
-    op("g", lambda: g.iota(T.jf[:], [[1, C]], C, 0, allow_small_or_imprecise_dtypes=True), [], ["jf"])
-    op("g", lambda: g.iota(T.ai[:], [[1, C]], 256, -1), [], ["ai"])
+    op("g", lambda: g.iota(T.ai[:], [[1, 128]], 256, -1), [], ["ai"])
 
     fill(T.co[:], 0.0, ["co"])
     fill(T.d12[:], 1.0, ["d12"])
     fill(T.z16[:], 0.0, ["z16"])
     fill(T.ft[:], 0.0, ["ft"])
+    fill(T.cs[:], 0.0, ["cs"])
     ts(T.pi[:, 1:2], T.pi[:, 0:1], 15, None, A.bitwise_and, None, ["pi0"], ["pi1"])
     ts(T.pi[:, 2:3], T.pi[:, 0:1], 4, 1, A.logical_shift_right, A.bitwise_and, ["pi0"], ["pi2"])
     cp(T.uo[:], T.ui[:], ["ui"], ["uo"])
-    R1, R320, HH = T.pf[:, 0:1], T.pf[:, 1:2], T.pf[:, 2:3]
+    R1, R320, HH, Q320, NT1, J0 = (T.pf[:, i:i + 1] for i in range(6))
     ts(R1, T.pi[:, 1:2], 1.0, None, A.add, None, ["pi1"], ["R1"])
     ts(R320, T.pi[:, 1:2], float(C), None, A.add, None, ["pi1"], ["R320"])
     cp(HH, T.pi[:, 2:3], ["pi2"], ["HH"])
     fill(T.co[:, 4 * SL + 33:4 * SL + 34], -2.0 ** -25, ["co"])
-    fill(T.co[:, 5 * SL + 32:5 * SL + 33], 2.0 ** -25, ["co"])
+    fill(T.co[:, 5 * SL + 32:5 * SL + 33], 2.0 ** -24, ["co"])
     ts(T.f2[:], T.jf[:, 0:16], R320, 1.0, A.is_le, A.add, ["jf", "R320"], ["f2"])
     ts(T.mk0[:], T.jf[:, 0:32], float(C + 16), HH, A.is_ge, A.not_equal, ["jf", "HH"], ["mk0"])
     ts(T.f1[:], T.f2[:], 4095.0, -4094.0, A.mult, A.add, ["f2"], ["f1"])
     scan(T.t2[:], T.f2[:], T.z16[:], 1.0, A.mult, A.add, ["f2", "z16"], ["t2"])
     ts(T.mk[:], T.mk0[:], -1024.0, None, A.mult, None, ["mk0"], ["mk"])
     scan(T.t1[:], T.f1[:], T.z16[:], TAU, A.mult, A.add, ["f1", "z16"], ["t1"])
+    clear(0)
 
     act(T.d12[:, SL + 32:SL + 33], R1, AF.Identity, ["R1"], ["d12"], scale=1.0 / 16, bias=1.0)
     for k in range(4):
         act(T.co[:, k * SL + 32:k * SL + 33], R1, AF.Identity, ["R1", "co"], ["co%d" % k], scale=2.0 ** (-8 - 4 * k))
     act(T.co[:, 4 * SL + 34:4 * SL + 35], R1, AF.Identity, ["R1", "co"], ["co4"], scale=2.0 ** -23)
+    act(T.cs[:, 32:33], R1, AF.Identity, ["R1", "cs"], ["cs0"], scale=FP / 1024.0, bias=-FP / 1024.0)
     act(T.d12[:, 32:33], T.t2[:, 15:16], AF.Identity, ["t2"], ["d12"])
+    act(NT1, T.t1[:, 15:16], AF.Identity, ["t1"], ["nt1"], scale=-1.0)
 
     quant(T.uq[:], T.us[:], T.ut[:], ["ut"], ["uq"])
     cp(T.uq2[:].bitcast(dt.uint32), T.uq[:].bitcast(dt.uint32).indirect(T.uo[:]), ["uq", "uo"], ["uq2"])
     act(T.us2[:], T.us[:].indirect(T.uo[:]), AF.Copy, ["uq", "uo"], ["us2"])
 
+    def equant(b):
+        quant(T.eq[:, 128 * b:128 * b + 128], T.es[:, 128 * b:128 * b + 128], T.eb[:, 3 - b:515 - b], ["e+"], ["eq%d" % b])
+
     def extras(k):
         if k == 0:
             fill(T.eb[:], 0.0, ["eb"])
-            fill(T.onm[:, 2:F + 2], -1.0, ["onm"])
+            fill(T.md[:, 0:GW], -1.0, ["md0"])
+            fill(T.gl[:, GW:GW + 32], 0.0, ["glt"])
+        if k == 1:
+            op("g", lambda: g.iota(T.jm[:], [[0, CP], [1, 16]], 1, 0, allow_small_or_imprecise_dtypes=True), [], ["jm"])
+            op("g", lambda: g.iota(T.jv[:], [[1, CP], [CP, 16]], -(C // 2), 0, allow_small_or_imprecise_dtypes=True), [], ["jv"])
+            cp(T.md[:, GW:GW + 1], T.mk[:, 0:1], ["mk"], ["md1"])
+            tt(T.md[:, GW + 1:GW + 32], T.mk[:, 1:32], T.mk[:, 0:31], A.subtract, ["mk"], ["md2"])
+            ts(Q320, HH, 16.0, R320, A.mult, A.add, ["HH", "R320"], ["Q320"])
         if k == 2:
-            act(T.jv[:], T.jf[:], AF.Identity, ["jf"], ["jv"], bias=-480.0)
+            ts(T.eb[:, 3:515:4], T.ai[:], 256.0, 64.0, A.is_equal, A.mult, ["ai", "eb"], ["e+"])
+            ts(T.eb[:, 523:1035:4], T.ai[:], 256.0, -64.0, A.is_equal, A.mult, ["ai", "eb"], ["e-"])
+            ts(T.sm[:], T.mk0[:], -2.0 ** -10, 2.0 ** -10, A.mult, A.add, ["mk0"], ["sm"])
+            ts(T.tg[:], T.jf[:], Q320, None, A.is_gt, None, ["jf", "Q320"], ["tg"])
+            fill(T.ha[:, 0:3 * CP:3], 0.0, ["ha0"])
+            act(J0, R1, AF.Identity, ["R1"], ["J0"], scale=float(CP), bias=float(-CP))
         if k == 3:
-            act(T.jc[:], T.jf[:], AF.Identity, ["jf"], ["jc"], scale=4.0, bias=-1598.0)
-            ts(T.eb[:, 3:515:4], T.ai[:, 0:128], 256.0, 64.0, A.is_equal, A.mult, ["ai", "eb"], ["e+"])
-            ts(T.eb[:, 523:1035:4], T.ai[:, 0:128], 256.0, -64.0, A.is_equal, A.mult, ["ai", "eb"], ["e-"])
-            fill(T.onm[:, 0:1], float(C), ["onm0"])
-            fill(T.onm[:, 1:2], 0.0, ["onm1"])
+            equant(0)
+            equant(1)
+            tt(T.me[:], T.tg[:], T.sm[:], A.mult, ["tg", "sm"], ["me"])
         if k == 4:
-            act(T.c2[:], T.jf[:], AF.Identity, ["jf"], ["c2"], scale=2.0, bias=-640.0)
-        if k == 5:
-            for b in range(4):
-                quant(T.eq[:, 128 * b:128 * b + 128], T.es[:, 128 * b:128 * b + 128], T.eb[:, 3 - b:515 - b], ["e+"], ["eq%d" % b])
+            equant(2)
+            equant(3)
+            tt(T.ml2[:], T.me[:], T.sm[:], A.subtract, ["me", "sm"], ["ml2"])
+            ts(T.hb[:, 0:3 * CP:3], T.jf[:, 0:CP], J0, 1.0 / PL, A.add, A.mult, ["jf", "J0"], ["hb0"])
             op("y", lambda: Y.dma_start(T.vt[:], T.v[:]), ["eq3"], ["vt"], sem="ldv", step=16)
             op("y", lambda: Y.dma_start(T.wq[:].bitcast(dt.uint8), T.wc[:]), [], ["wq"], sem="ldw", step=16, total=32)
             op("y", lambda: Y.dma_start(T.wp[:], T.ws[:]), [], ["wp"], sem="ldw", step=16, total=32)
-        if k == 7:
-            ts(T.a2[:], T.ai[:], 15, None, A.bitwise_and, None, ["ai"], ["a2"])
-            fill(T.sw0[:, 0:C], -256.0, ["sw0"])
-            ts(T.cw[:], T.jf[:, 0:C:16], R1, 2.0, A.add, A.mult, ["jf", "R1"], ["cw"])
-            fill(T.slt[:, 0:2], 0.0, ["sltp"])
+        if k == 5:
+            fill(T.hb[:, 1:3 * CP:3], 1.0, ["hb1"])
+        if k == 6:
+            fill(T.fg[:, 32:PE + 33:PE], 0.0, ["fgp"])
         if k == 8:
-            ts(T.dmp[:], T.a2[:], 0.0, 2048.0, A.is_equal, A.mult, ["a2"], ["dmp"])
-            fill(T.nle[:, 0:2], 0.0, ["nlep"])
-            ts(T.dmn[:], T.dmp[:], -1.0, None, A.mult, None, ["dmp"], ["dmn"])
+            ts(T.dmp[:], T.jm[:], R1, 2048.0, A.is_equal, A.mult, ["jm", "R1"], ["dmp"])
         if k == 9:
             for b in (2, 3):
                 quant(T.eq[:, 256 + 128 * b:384 + 128 * b], T.es[:, 256 + 128 * b:384 + 128 * b], T.eb[:, 523 - b:1035 - b], ["e-"], ["eq%d" % (2 + b)])
-        if k == 10:
-            fill(T.md[:, 0:GW], -1.0, ["md0"])
-            fill(T.gl[:, GW:GW + 32], 0.0, ["glt"])
-            cp(T.md[:, GW:GW + 1], T.mk[:, 0:1], ["mk"], ["md1"])
-            tt(T.md[:, GW + 1:GW + 32], T.mk[:, 1:32], T.mk[:, 0:31], A.subtract, ["mk"], ["md2"])
 
     def lo(k):
         return T.rr[:, (k - 1) * SL + 31:(k - 1) * SL + 32]
@@ -256,7 +278,7 @@ def rank_program(g, core, T, topo):
         h1, h2, h3 = helpers(core, other, topo)
         tq, tsc, pq, psc = T["tq%d" % t], T["ts%d" % t], T["pq%d" % t], T["ps%d" % t]
         ao, la, sw = T["ao%d" % t], T["la%d" % t], T["sw%d" % t]
-        ktq, kao, ksw = "tq%d" % t, "ao%d" % t, "sw%d" % t
+        ktq, kao, ksw = "tq%d" % t, "ao%d" % t, ["swa%d" % t, "swb%d" % t]
         bulk, lst = T.sem["bulk%d" % t], T.sem["lst%d" % t]
         if t == 0:
             quant(tq[:], tsc[:], T.xt[:], ["xt"], [ktq])
@@ -285,6 +307,7 @@ def rank_program(g, core, T, topo):
         mx(1, T.uq2[:, 128:256], T.us2[:, 128:256], tq[:], tsc[:], True, True, ["uq2", "us2", ktq])
         B, HI = T.xx[:, 0:C], T.xx[:, C:F]
         t1 = T.t1[:, 15:16]
+        s0 = T.sc[:, 0:1]
         if t == 0:
             act(B, bank(0), AF.Relu, ["bk0"], ["B"], scale=-1.0)
         else:
@@ -293,41 +316,48 @@ def rank_program(g, core, T, topo):
         act(T.ab[:], bank(1), AF.Abs, ["bk1"], ["ab"])
         tt(HI, B, T.ab[:], A.add, ["B", "ab"], ["HI"])
         if t > 0:
-            act(T.r0[:], bank(1), AF.Relu, ["bk1"], ["r0"], scale=-1.0)
-        act(T.junk[:, 0:C], B, AF.Sign, ["B", "t1"], ["j0", "s0"], scale=-1.0, bias=t1, accum_out=T.sc[:, 0:1])
+            act(T.rv[:, 0:F:2], bank(1), AF.Relu, ["bk1"], ["r0"], scale=-1.0)
+        act(T.junk[:, 0:C], B, AF.Sign, ["B", "nt1"], ["j0", "s0"], bias=NT1, accum_out=s0)
         if t == 0:
-            act(T.r0[:], bank(1), AF.Relu, ["bk1"], ["r0"], scale=-1.0)
-        ts(T.mk2[:], T.mk[:], T.sc[:, 0:1], None, A.subtract, None, ["mk", "s0"], ["mk2"])
+            act(T.rv[:, 0:F:2], bank(1), AF.Relu, ["bk1"], ["r0"], scale=-1.0)
+            ts(T.mk2[:], T.mk[:], s0, None, A.add, None, ["mk", "s0"], ["mk2"])
 
         thr, kthr = t1, "t1"
+        nb = T.dd[:, 4 * SL + 32:4 * SL + 33]
         for k in range(1, 9):
             sk = T.sc[:, k:k + 1]
-            d = SHARE.get(k, 0) if t > 0 else 0
-            src, ksrc = (T.xx, ["B", "HI"]) if k < 8 else (T.dv, ["dv"])
+            d = (SHARE if t > 0 else SHARE0).get(k, 0)
             if k == 1:
-                act(T.junk[:, C:F], HI, AF.Sign, ["HI", kthr], ["j1", "s1"], scale=-1.0, bias=thr, accum_out=sk)
-                act(T.r1[:], bank(1), AF.Relu, ["bk1"], ["r1"])
+                act(T.junk[:, C + d:F], T.xx[:, C + d:F], AF.Sign, ["HI", kthr], ["j1", "s1"], scale=-1.0, bias=thr, accum_out=sk)
+                act(T.rv[:, 1:F:2], bank(1), AF.Relu, ["bk1"], ["r1"])
+                op("y", lambda: Y.dma_start(T.bd[:], T.xx[0:128:16, 0:C]), ["B", "HI"], ["bd"], sem="deal", step=16, total=32 * (t + 1))
+                op("y", lambda: Y.dma_start(T.rd[:], T.rv[0:128:16, :]), ["r0", "r1"], ["rd"], sem="deal", step=16, total=32 * (t + 1))
+                vsrc, ksrc = T.xx[:, C:C + d], ["HI"]
             else:
+                src, ksrc = (T.xx, ["B", "HI"]) if k < 8 else (T.dv, ["dv0", "dv1"])
                 act(T.junk[:, d:F], src[:, d:F], AF.Sign, ksrc + [kthr], ["j0", "j1", "s%d" % k], scale=-1.0, bias=thr, accum_out=sk)
+                vsrc = src[:, 0:d]
             if d:
-                ts(T.gl[:, GW - d:GW], src[:, 0:d], thr, 2.0, A.is_gt, A.mult, ksrc + [kthr], ["gl"])
-            if k == 2:
-                tt(T.ci[:, 0:F:2], B, T.r0[:], A.add, ["B", "r0"], ["c0"])
+                ts(T.gl[:, GW - d:GW], vsrc, thr, 2.0, A.is_gt, A.mult, ksrc + [kthr], ["gl"])
             if k == 3:
                 ts(T.dd[:], T.co[:], lo(2), None, A.mult, None, ["co", "co0", "co1", "co2", "co3", "co4", "rr2"], ["dd", "nb"])
             if k == 4:
-                tt(T.ci[:, 1:F:2], B, T.r1[:], A.add, ["B", "r1"], ["c1"])
-            nb = T.dd[:, 4 * SL + 32:4 * SL + 33]
-            if k == 5:
                 ts(nb, lo(2), 2.0 ** -8, lo(3), A.mult, A.subtract, ["rr2", "rr3"], ["nb"])
-            if k == 6:
-                ts(T.dv[:], T.ci[:], TAU, nb, A.max, A.add, ["c0", "c1", "nb"], ["dv"])
+            if k in (5, 6):
+                a = C * (k - 5)
+                ts(T.dv[:, a:a + C], T.xx[:, a:a + C], TAU, nb, A.max, A.add, ["B", "HI", "nb"], ["dv%d" % (k - 5)])
+            if k == 7:
+                tt(T.cd[:, 0:FP:2], T.bd[:], T.rd[:, 0:FP:2], A.add, ["bd", "rd"], ["cd0"])
+                tt(T.cd[:, 1:FP:2], T.bd[:], T.rd[:, 1:FP:2], A.add, ["bd", "rd"], ["cd1"])
+            if k == 8:
+                ts(T.dvd[:], T.cd[:], TAU, nb, A.max, A.add, ["cd0", "cd1", "nb"], ["dvd"])
             if t == 0:
                 extras(k)
             if d:
-                scan(T.mo[:, GW - d:GW + 32], T.gl[:, GW - d:GW + 32], T.md[:, GW - d:GW + 32], 0.0, A.add, A.add,
-                     ["gl", "glt", "md0", "md1", "md2"], ["mo"])
-                mask, kmask = T.mo[:, GW:GW + 32], "mo"
+                mo = T.mo1 if k == 1 else T.mo
+                scan(mo[:, GW - d:GW + 32], T.gl[:, GW - d:GW + 32], T.md[:, GW - d:GW + 32], s0 if k == 1 else 0.0, A.add, A.add,
+                     ["gl", "glt", "md0", "md1", "md2"] + (["s0"] if k == 1 else []), ["mo"])
+                mask, kmask = mo[:, GW:GW + 32], "mo"
             elif k == 1:
                 mask, kmask = T.mk2[:], "mk2"
             else:
@@ -349,18 +379,25 @@ def rank_program(g, core, T, topo):
             scan(T.rr[:, o:o + w], T.ft[:, 0:w], d1, init, A.max, o1, ["ft"] + kd + ki, ["rr%d" % k])
             thr, kthr = T.rr[:, o + w - 1:o + w], "rr%d" % k
 
-        act(T.slt[:, 2:F + 2], T.dv[:], AF.Sign, ["dv", "rr8"], ["slt", "s9"], scale=-1.0, bias=lo(8), accum_out=T.sc[:, 9:10])
-        ts(T.nle[:, 2:F + 2], T.dv[:], thr, -2.0, A.is_le, A.mult, ["dv", "rr8"], ["nle"])
-        scan(T.yy[:], T.onm[:], T.slt[:], T.sc[:, 9:10], A.add, A.subtract, ["onm", "onm0", "onm1", "slt", "sltp", "s9"], ["yy"])
-        scan(T.kk[:], T.nle[:], T.yy[:], float(C), A.add, A.max, ["nle", "nlep", "yy"], ["kk"])
-        scan(T.ga[:], T.dmn[:], T.kk[:, 1:F + 1:2], 0.0, A.add, A.max, ["dmn", "kk"], ["ga"])
-        scan(T.gb[:], T.dmn[:], T.kk[:, 3:F + 2:2], 0.0, A.add, A.max, ["dmn", "kk"], ["gb"])
-        tt(T.e1[:], T.ga[:, 15:C:16], T.gb[:, 15:C:16], A.is_equal, ["ga", "gb"], ["e1"])
-        tt(T.e2[:], T.e1[:], T.cw[:], A.mult, ["e1", "cw"], ["e2"])
-        tt(T.e3[:], T.e2[:], T.ga[:, 15:C:16], A.subtract, ["e2", "ga"], ["e3"])
-        ts(T.so[:], T.e3[:], float(C), 0.5, A.add, A.mult, ["e3"], ["so"])
-        cp(sw[:, 0:976].indirect(T.so[:]), T.jv[:], ["so", "jv"], [ksw])
-        scan(T.fi[:], sw[:, 0:C], sw[:, 0:C], -256.0, A.max, A.max, [ksw], ["fi"])
+        act(T.jk2[:, 0:FP], T.dvd[:], AF.Sign, ["dvd", "rr8"], ["jk0", "s9"], scale=-1.0, bias=lo(8), accum_out=T.sc[:, 9:10])
+        act(T.jk2[:, FP:2 * FP], T.dvd[:], AF.Sign, ["dvd", "rr8"], ["jk1", "s10"], scale=-1.0, bias=thr, accum_out=T.sc[:, 10:11])
+        ts(T.fg[:, 33:PW], T.dvd[:], lo(8), 1.0 / PL, A.is_lt, A.mult, ["dvd", "rr8"], ["fg0"])
+        ts(T.fg[:, PE + 33:PE + PW], T.dvd[:], thr, 1.0 / PL, A.is_lt, A.mult, ["dvd", "rr8"], ["fg1"])
+        ts(T.fl2[:, 0:32], T.ml2[:], T.sc[:, 9:10], None, A.mult, None, ["ml2", "s9"], ["fl20"])
+        ts(T.fl2[:, 32:64], T.me[:], T.sc[:, 10:11], None, A.mult, None, ["me", "s10"], ["fl21"])
+        op("v", lambda: V.transpose(T.fg[:, 0:32], T.fl2[:, 0:32]), ["fl20"], ["fa0"])
+        op("v", lambda: V.transpose(T.fg[:, PE:PE + 32], T.fl2[:, 32:64]), ["fl21"], ["fa1"])
+        kc = ["cs", "cs0", "fgp"]
+        scan(T.kt[:, 0:PW], T.fg[:, 0:PW], T.cs[:, 0:PW], 0.0, A.add, A.add, ["fg0", "fa0"] + kc, ["kt"])
+        scan(T.ke[:, 0:PW], T.fg[:, PE:PE + PW], T.cs[:, 0:PW], 0.0, A.add, A.add, ["fg1", "fa1"] + kc, ["ke"])
+        tt(T.kk[:, 0:FP + 1], T.kt[:, 32:PW], T.ke[:, 32:PW], A.min, ["kt", "ke"], ["kk"])
+        tt(T.hb[:, 2:3 * CP:3], T.kt[:, 32:PW - 1:2], T.ke[:, 32:PW - 1:2], A.min, ["kt", "ke"], ["hb2"])
+        tt(T.ha[:, 1:3 * CP:3], T.kk[:, 2:FP + 1:2], T.kk[:, 1:FP:2], A.is_equal, ["kk"], ["ha1"])
+        tt(T.ha[:, 2:3 * CP:3], T.kk[:, 1:FP:2], T.kk[:, 0:FP:2], A.is_equal, ["kk"], ["ha2"])
+        scan(T.hs[:], T.ha[:], T.hb[:], 0.0, A.mult, A.add, ["ha0", "ha1", "ha2", "hb0", "hb1", "hb2"], ["hs"])
+        ts(T.so[:], T.hs[:, 2:3 * CP:3], float(PL), None, A.mult, None, ["hs"], ["so"])
+        cp(sw[:, 0:SW].indirect(T.so[:]), T.jv[:], ["so", "jv"], ksw)
+        scan(T.fi[:], sw[:, 0:C], sw[:, PL:PL + C], -256.0, A.max, A.max, ksw, ["fi"])
         scan(T.gf[:], T.dmp[:], T.fi[:], 0.0, A.add, A.min, ["dmp", "fi"], ["gf"])
         ts(ao[:], T.gf[:, 15:C:16], float(H), None, A.add, None, ["gf"], [kao])
         op("g", lambda: g.remote_dma(la[:], ao[:], lst, T.sem.sent, pid2, rid2, bits(eng)), [kao], [], step=0)
@@ -374,21 +411,19 @@ def rank_program(g, core, T, topo):
         for b in range(4):
             act(T.dp[:, C * b:C * b + C], bank(4 + b), AF.Identity, ["bk%d" % (4 + b)], ["dp%d" % b], scale=1.0 / 64)
 
-        tt(T.xw[:], T.kk[:, 2:F + 2:2], T.jc[:], A.add, ["kk", "jc"], ["xw"])
+        act(T.bg[:], T.xx[:, 0:C].indirect(ao[:]), AF.Copy, ["B", kao], ["bg"])
+        ts(T.bt[:], sw[:, 0:C], -256.0, 0.5, A.is_equal, A.mult, ksw, ["bt"])
         if t == 0:
             extras(9)
-        tt(T.k2[:], T.xw[:].indirect(ao[:]), T.c2[:], A.add, ["xw", kao, "c2"], ["k2"])
-        scan(T.gk[:], T.dmp[:], T.k2[:], 0.0, A.add, A.min, ["dmp", "k2"], ["gk"])
-        if t + 1 < ROUNDS:
-            fill(T["sw%d" % (t + 1)][:, 0:C], -256.0, ["sw%d" % (t + 1)])
-        ts(T.ko[:], T.gk[:, 15:C:16], 0.5, None, A.mult, None, ["gk"], ["ko"])
-        act(T.mm[:], T.ci[:].indirect(T.ko[:]), AF.Copy, ["c0", "c1", "ko"], ["mm"])
-        if t == 0:
-            extras(10)
+        tt(T.kh[:], T.fi[:], T.bt[:], A.add, ["fi", "bt"], ["kh"])
+        scan(T.gk[:], T.dmp[:], T.kh[:], 0.0, A.add, A.min, ["dmp", "kh"], ["gk"])
         if t == 1:
             quant(T.vq[:], T.vs[:], T.vt[:], ["vt"], ["vq"])
         if t == ROUNDS - 1:
-            ts(T.kf[:], T.k2[:], 0.5, None, A.mult, None, ["k2"], ["kf"])
+            ts(T.kf[:], T.kh[:], 2.0, float(C), A.mult, A.add, ["kh"], ["kf"])
+        ts(T.ko[:], T.gk[:, 15:C:16], 2.0, float(C), A.mult, A.add, ["gk"], ["ko"])
+        tt(T.mm[:], T.rv[:].indirect(T.ko[:]), T.bg[:], A.add, ["r0", "r1", "ko", "bg"], ["mm"])
+        if t == ROUNDS - 1:
             op("y", lambda: Y.dma_start(T.kl[:], T.kf[0:128:16, :]), ["kf"], [], sem="stk", step=16)
             op("y", lambda: Y.dma_start(T.ml[:], T.mm[0:128:16, :]), ["mm"], [], sem="stk", step=16)
         for b in (2, 3):
@@ -400,6 +435,8 @@ def rank_program(g, core, T, topo):
         for b in (2, 3):
             act(T.zt[:, b:4 * C:4], T.dp[:, C * b:C * b + C].indirect(la[:]), AF.Copy, ["dp%d" % b, "la"], ["zt%d" % b])
         quant(T.zq[:], T.zs[:], T.zt[:], ["zt0", "zt1", "zt2", "zt3"], ["zq"])
+        if t + 1 < ROUNDS:
+            clear(t + 1)
         for b, bk in ((0, 0), (2, 4), (2, 5), (1, 1), (3, 6), (3, 7)):
             mx(bk, T.wq[:, 128 * b:128 * b + 128], T.wp[:, 128 * b:128 * b + 128], T.zq[:], T.zs[:], b < 2, True, ["wq", "wp", "zq"])
 
@@ -418,13 +455,10 @@ def rank_program(g, core, T, topo):
             else:
                 act(out, win, AF.Copy, rd, wr)
 
-        for b in (0, 2):
+        for b in range(4):
             child(b, 0)
             child(b, 1)
-            child(b + 1, 0)
             pick(b)
-            child(b + 1, 1)
-            pick(b + 1)
 
     tq, tsc, ktq = T["tq%d" % ROUNDS], T["ts%d" % ROUNDS], "tq%d" % ROUNDS
     quant(tq[:], tsc[:], T.tt[:], ["tt0", "tt1", "tt2", "tt3"], [ktq])
@@ -435,5 +469,5 @@ def rank_program(g, core, T, topo):
     act(T.yo[:], bank(0), AF.Copy, ["bk0"], ["yo"])
     op("a", lambda: S.dma_start(T.y[:], T.yo[:]), ["yo"], [], sem="sty", step=16)
     g.wait_ge(T.sem.sent, sent)
-    for s in ("sg", "sv", "sp", "sa", "stk", "sto", "sty"):
+    for s in ("sg", "sv", "sp", "sa", "stk", "sto", "sty", "deal"):
         g.wait_ge(T.sem[s], count[s])

@@ -1,40 +1,41 @@
 from concourse.bass import DstId, RemoteDMATransfer
-from concourse.mybir import dt, AluOpType, ActivationFunctionType
+from concourse.mybir import dt, AluOpType, ActivationFunctionType, AxisListType
 
 C = 320
 F = 2 * C
+H = C // 2
 ROUNDS = 3
 PARTNER = [1, 2, 4]
 TAU = 2.0 ** -100
-SL = 36
-GW = 192
-SHARE = {1: 64, 2: 192, 3: 144, 4: 192, 5: 112, 6: 112, 7: 144, 8: 192}
-SHARE0 = {5: 112, 6: 112, 7: 144, 8: 144}
+BIG = 2.0 ** 99
+GW = 224
+SHARE = {2: 176, 3: 176, 4: 224, 5: 224, 6: 224, 7: 224, 8: 224}
 CP = C // 16
 FP = 2 * CP
-PW = 32 + 1 + FP
-PE = 76
 PL = 512
-SW = PL + 3 * C
+JW = 2 * C + 64
+SW = PL + 2 * C + 16 * JW
+UO = 62
+ZA = 160
+TA = [160, 192, 192, 192]
 Q4 = "float8_e4m3fn_x4"
 
 SCRATCH = {}
 for _dt, _list in (
-    ("bfloat16", (("xt", 4 * C), ("tt", 4 * C), ("ut", 512), ("vt", 512), ("eb", 1040), ("zt", 4 * C), ("dp", 4 * C), ("dn", 2 * C),
-                  ("tw", 4 * F), ("junk", F), ("jk2", 2 * FP), ("dmp", C), ("jv", C), ("jm", C), ("fi", C), ("gf", C), ("bt", C),
-                  ("gl", GW + 32), ("md", GW + 32), ("mo", GW + 32), ("sw0", SW), ("sw1", SW), ("sw2", SW))),
-    ("float32", (("pf", 8), ("jf", 32), ("f1", 16), ("f2", 16), ("t1", 16), ("t2", 16), ("z16", 16), ("mk0", 32), ("mk", 32), ("mk2", 32),
-                 ("d12", 2 * SL), ("co", 6 * SL), ("dd", 6 * SL), ("fl", 32), ("ft", SL), ("rr", 8 * SL), ("sc", 16),
-                 ("nz", C), ("ab", C), ("rv", F), ("xx", F), ("dv", F), ("mm", C), ("bg", C), ("mo1", GW + 32),
-                 ("bd", CP), ("rd", FP), ("cd", FP), ("dvd", FP), ("fg", 2 * PE), ("cs", PE), ("ke", PE), ("kt", PE), ("kk", 44),
-                 ("sm", 32), ("tg", 32), ("me", 32), ("ml2", 32), ("fl2", 64),
-                 ("ha", 3 * CP), ("hb", 3 * CP), ("hs", 3 * CP),
+    ("bfloat16", (("xt", 4 * C), ("tt", 4 * C), ("ut", 512), ("vt", 512), ("eb", 520), ("zt", 4 * C), ("dp", 4 * C), ("dn", 4 * C),
+                  ("tw", 2 * F), ("hz", 2 * C), ("junk", F), ("jk2", 4 * FP), ("dmp", C), ("jv", C), ("jm", C), ("fi", C), ("gf", C), ("bt", C),
+                  ("gl", GW), ("mo", GW), ("pb", 2), ("sw", SW))),
+    ("float32", (("pf", 16), ("jf", 64), ("f1", 16), ("f2", 16), ("fh", 16), ("t1", 16), ("t2", 16), ("t3", 16), ("tl", 16), ("k16", 16),
+                 ("z16", 16), ("mk0", 32), ("tg", 32), ("w1", 32), ("w2", 32), ("co", 48), ("dd", 48), ("th", 16), ("sc", 16), ("j16", 16),
+                 ("nz", C), ("ab", C), ("rv", F), ("xx", F), ("dv", F), ("mm", C), ("bg", C), ("rw", 2 * F),
+                 ("bd", CP), ("rd", FP), ("cd", FP), ("dq", 4 * FP), ("mb", 64), ("fl", 64), ("fg", 66 + 2 * FP), ("pl", 33 + FP),
+                 ("ha", 4 * CP), ("hb", UO + 4 * CP + 4), ("hs", 4 * CP),
                  ("kh", C), ("gk", C), ("kf", C), ("yo", C))),
     ("int32", (("pi", 8), ("ui", 16), ("ai", 128))),
-    ("uint16", (("uo", 16), ("so", 20), ("ko", 20), ("ao0", 20), ("ao1", 20), ("ao2", 20), ("la0", 20), ("la1", 20), ("la2", 20))),
-    (Q4, (("uq", 128), ("uq2", 256), ("vq", 128), ("wq", 512), ("eq", 768), ("zq", C),
+    ("uint16", (("uo", 16), ("of", 16), ("so", 20), ("ko", 20), ("ao0", 20), ("ao1", 20), ("ao2", 20), ("la0", 20), ("la1", 20), ("la2", 20))),
+    (Q4, (("uq", 128), ("uq2", 256), ("vq", 128), ("wq", 512), ("eq", 512), ("zq", C),
           ("tq0", C), ("tq1", C), ("tq2", C), ("tq3", C), ("pq0", C), ("pq1", C), ("pq2", C))),
-    ("uint8", (("us", 128), ("us2", 256), ("vs", 128), ("wp", 512), ("es", 768), ("zs", C),
+    ("uint8", (("us", 128), ("us2", 256), ("vs", 128), ("wp", 512), ("es", 512), ("zs", C),
                ("ts0", C), ("ts1", C), ("ts2", C), ("ts3", C), ("ps0", C), ("ps1", C), ("ps2", C))),
 ):
     for _name, _n in _list:
@@ -42,7 +43,7 @@ for _dt, _list in (
 for _b in range(8):
     SCRATCH["bk%d" % _b] = ("psum", [128, 512], "float32")
 
-SEMAPHORES = (["sv", "sa", "sp", "sg", "sent", "ldu", "ldx", "ldv", "ldw", "stk", "sto", "sty", "deal"]
+SEMAPHORES = (["sv", "sa", "sp", "sg", "sent", "ldu", "ldxa", "ldxb", "ldv", "ldw", "stk", "sto", "sty", "deal"]
               + ["bulk%d" % t for t in range(ROUNDS)] + ["lst%d" % t for t in range(ROUNDS)])
 
 A = AluOpType
@@ -65,7 +66,6 @@ def helpers(me, other, topo):
 
 def helper_program(g, core, T, topo):
     sent = 0
-    H = C // 2
     for t in range(ROUNDS):
         for r, me in enumerate(T.cores):
             other = T.cores[r ^ PARTNER[t]]
@@ -167,59 +167,75 @@ def rank_program(g, core, T, topo):
     def act(out, in_, f, reads, writes, **kw):
         op("a", lambda: S.activation(out, in_, f, **kw), reads, writes)
 
+    def afill(ap, n, val, reads, writes):
+        act(ap, T.jf[:, 0:n], AF.Identity, ["jf"] + reads, writes, scale=0.0, bias=val)
+
+    def iota(out, pattern, base, cm, writes):
+        op("g", lambda: g.iota(out, pattern, base, cm, allow_small_or_imprecise_dtypes=True), [], writes)
+
     def quant(q, s, t, reads, writes):
         op("v", lambda: V.quantize_mx(q, s, t), reads, writes)
 
-    def mx(bank, lq, ls, rq, rs, start, stop, reads):
-        op("p", lambda: P.matmul_mx(T["bk%d" % bank][:, 0:C], lq, ls, rq, rs, start, stop), reads, ["bk%d" % bank])
+    def bank(b, n=C):
+        return T["bk%d" % b][:, 0:n]
 
-    def bank(b):
-        return T["bk%d" % b][:, 0:C]
+    def mx(b, n, lq, ls, rq, rs, reads):
+        op("p", lambda: P.matmul_mx(bank(b, n), lq, ls, rq, rs, True, True), reads, ["bk%d" % b])
 
-    def unit(bk, e, q, s, stop, reads):
-        mx(bk, T.eq[:, 128 * e:128 * e + 128], T.es[:, 128 * e:128 * e + 128], q[:], s[:], True, stop, ["eq%d" % e] + reads)
+    def unit(bk, e, q, s, reads):
+        mx(bk, C, T.eq[:, 128 * e:128 * e + 128], T.es[:, 128 * e:128 * e + 128], q[:], s[:], ["eq%d" % e] + reads)
 
-    def clear(t):
-        fill(T["sw%d" % t][:, 0:C], -256.0, ["swa%d" % t])
-        fill(T["sw%d" % t][:, PL:PL + C], -256.0, ["swb%d" % t])
+    def parts(a):
+        return ((0, a), (a, C))
 
+    xa = 4 * TA[0]
     op("y", lambda: Y.dma_start(T.ut[:], T.u[:]), [], ["ut"], sem="ldu", step=16)
-    op("a", lambda: S.dma_start(T.xt[:], T.x[:]), [], ["xt"], sem="ldx", step=16)
+    op("a", lambda: S.dma_start(T.xt[:, 0:xa], T.x[:, 0:xa]), [], ["xt0"], sem="ldxa", step=16)
+    op("y", lambda: Y.dma_start(T.xt[:, xa:4 * C], T.x[:, xa:4 * C]), [], ["xt1"], sem="ldxb", step=16)
 
     op("g", lambda: g.iota(T.pi[:, 0:1], [[0, 1]], 0, 1), [], ["pi0"])
-    op("g", lambda: g.iota(T.jf[:], [[1, 32]], C, 0, allow_small_or_imprecise_dtypes=True), [], ["jf"])
+    iota(T.jf[:], [[1, 64]], C, 0, ["jf"])
     op("g", lambda: g.iota(T.ui[:], [[-1, 2], [16, 8]], 1, 0), [], ["ui"])
     op("g", lambda: g.iota(T.ai[:], [[1, 128]], 256, -1), [], ["ai"])
+    iota(T.jm[:], [[0, CP], [1, 16]], 1, 0, ["jm"])
+    iota(T.jv[:], [[1, CP], [CP, 16]], -H, 0, ["jv"])
 
-    fill(T.co[:], 0.0, ["co"])
-    fill(T.d12[:], 1.0, ["d12"])
+    R1, R320, HH, NQ, NT1, J2, JZ, C3, RM, KAP, JJ = (T.pf[:, i:i + 1] for i in range(11))
+    I0 = T.fg[:, 0:1]
+    P2, K2 = T.t2[:, 15:16], T.t3[:, 15:16]
+    fill(T.k16[:], 4096.0, ["k16"])
     fill(T.z16[:], 0.0, ["z16"])
-    fill(T.ft[:], 0.0, ["ft"])
-    fill(T.cs[:], 0.0, ["cs"])
+    fill(T.co[:], 0.0, ["co"])
+    fill(T.w1[:], 0.0, ["w1"])
     ts(T.pi[:, 1:2], T.pi[:, 0:1], 15, None, A.bitwise_and, None, ["pi0"], ["pi1"])
     ts(T.pi[:, 2:3], T.pi[:, 0:1], 4, 1, A.logical_shift_right, A.bitwise_and, ["pi0"], ["pi2"])
-    cp(T.uo[:], T.ui[:], ["ui"], ["uo"])
-    R1, R320, HH, Q320, NT1, J0 = (T.pf[:, i:i + 1] for i in range(6))
+    scan(T.tl[:], T.k16[:], T.z16[:], TAU, A.mult, A.add, ["k16", "z16"], ["tl"])
     ts(R1, T.pi[:, 1:2], 1.0, None, A.add, None, ["pi1"], ["R1"])
     ts(R320, T.pi[:, 1:2], float(C), None, A.add, None, ["pi1"], ["R320"])
     cp(HH, T.pi[:, 2:3], ["pi2"], ["HH"])
-    fill(T.co[:, 4 * SL + 33:4 * SL + 34], -2.0 ** -25, ["co"])
-    fill(T.co[:, 5 * SL + 32:5 * SL + 33], 2.0 ** -24, ["co"])
+    fill(T.w2[:], 0.0, ["w2"])
     ts(T.f2[:], T.jf[:, 0:16], R320, 1.0, A.is_le, A.add, ["jf", "R320"], ["f2"])
-    ts(T.mk0[:], T.jf[:, 0:32], float(C + 16), HH, A.is_ge, A.not_equal, ["jf", "HH"], ["mk0"])
+    cp(T.uo[:], T.ui[:], ["ui"], ["uo"])
+    fill(T.j16[:], 2.0, ["j16"])
     ts(T.f1[:], T.f2[:], 4095.0, -4094.0, A.mult, A.add, ["f2"], ["f1"])
     scan(T.t2[:], T.f2[:], T.z16[:], 1.0, A.mult, A.add, ["f2", "z16"], ["t2"])
-    ts(T.mk[:], T.mk0[:], -1024.0, None, A.mult, None, ["mk0"], ["mk"])
+    scan(T.w2[:, 1:32:2], T.j16[:], T.z16[:], 0.5, A.mult, A.add, ["j16", "z16", "w2"], ["w2"])
     scan(T.t1[:], T.f1[:], T.z16[:], TAU, A.mult, A.add, ["f1", "z16"], ["t1"])
-    clear(0)
+    ts(T.w1[:, 1:32:2], T.tl[:], P2, None, A.mult, None, ["tl", "t2", "w1"], ["w11"])
 
-    act(T.d12[:, SL + 32:SL + 33], R1, AF.Identity, ["R1"], ["d12"], scale=1.0 / 16, bias=1.0)
-    for k in range(4):
-        act(T.co[:, k * SL + 32:k * SL + 33], R1, AF.Identity, ["R1", "co"], ["co%d" % k], scale=2.0 ** (-8 - 4 * k))
-    act(T.co[:, 4 * SL + 34:4 * SL + 35], R1, AF.Identity, ["R1", "co"], ["co4"], scale=2.0 ** -23)
-    act(T.cs[:, 32:33], R1, AF.Identity, ["R1", "cs"], ["cs0"], scale=FP / 1024.0, bias=-FP / 1024.0)
-    act(T.d12[:, 32:33], T.t2[:, 15:16], AF.Identity, ["t2"], ["d12"])
+    for k in range(3, 9):
+        afill(T.co[:, 8 * k - 23:8 * k - 22], 1, 2.0 ** (8 - 4 * k) if k < 8 else 2.0 ** -23, ["co"], ["coa%d" % k])
+    afill(T.co[:, 44:45], 1, 2.0 ** -24, ["co"], ["cod"])
+    act(C3, R1, AF.Identity, ["R1"], ["C3"], scale=1.0 / 16, bias=1.0)
+    act(RM, R1, AF.Identity, ["R1"], ["RM"], scale=-15.0 / 16)
+    act(J2, R1, AF.Identity, ["R1"], ["J2"], scale=2.0, bias=-2.0)
+    act(T.co[:, 34:35], R1, AF.Identity, ["R1", "co"], ["cob7"], scale=2.0 ** -23 - 2.0 ** -20, bias=-2.0 ** -24)
+    act(T.co[:, 42:43], R1, AF.Identity, ["R1", "co"], ["cob8"], scale=-2.0 ** -23, bias=2.0 ** -25)
+    act(T.co[:, 2:32:8], T.co[:, 1:32:8], AF.Identity, ["RM", "coa3", "coa4", "coa5", "coa6"], ["cob"], scale=RM)
     act(NT1, T.t1[:, 15:16], AF.Identity, ["t1"], ["nt1"], scale=-1.0)
+    act(T.w1[:, 0:1], P2, AF.Identity, ["t2", "w1"], ["w10"], scale=TAU)
+    kcoa = ["coa%d" % k for k in range(3, 9)]
+    kco = ["co", "cod", "cob", "cob7", "cob8", "coc"] + kcoa
 
     quant(T.uq[:], T.us[:], T.ut[:], ["ut"], ["uq"])
     cp(T.uq2[:].bitcast(dt.uint32), T.uq[:].bitcast(dt.uint32).indirect(T.uo[:]), ["uq", "uo"], ["uq2"])
@@ -228,63 +244,130 @@ def rank_program(g, core, T, topo):
     def equant(b):
         quant(T.eq[:, 128 * b:128 * b + 128], T.es[:, 128 * b:128 * b + 128], T.eb[:, 3 - b:515 - b], ["e+"], ["eq%d" % b])
 
+    def clear(i):
+        fill(T.sw[:, PL * i:PL * i + C], -256.0, ["sw%d" % i])
+
     def extras(k):
         if k == 0:
+            ts(T.fh[:], T.f2[:], -0.5, 1.5, A.mult, A.add, ["f2"], ["fh"])
+            op("v", lambda: V.reciprocal(KAP, C3), ["C3"], ["KAP"])
+            scan(T.t3[:], T.fh[:], T.z16[:], C3, A.mult, A.add, ["fh", "z16", "C3"], ["K2"])
             fill(T.eb[:], 0.0, ["eb"])
-            fill(T.md[:, 0:GW], -1.0, ["md0"])
-            fill(T.gl[:, GW:GW + 32], 0.0, ["glt"])
-        if k == 1:
-            op("g", lambda: g.iota(T.jm[:], [[0, CP], [1, 16]], 1, 0, allow_small_or_imprecise_dtypes=True), [], ["jm"])
-            op("g", lambda: g.iota(T.jv[:], [[1, CP], [CP, 16]], -(C // 2), 0, allow_small_or_imprecise_dtypes=True), [], ["jv"])
-            cp(T.md[:, GW:GW + 1], T.mk[:, 0:1], ["mk"], ["md1"])
-            tt(T.md[:, GW + 1:GW + 32], T.mk[:, 1:32], T.mk[:, 0:31], A.subtract, ["mk"], ["md2"])
-            ts(Q320, HH, 16.0, R320, A.mult, A.add, ["HH", "R320"], ["Q320"])
-        if k == 2:
+        if k == -1:
+            ts(T.w2[:, 0:2], T.w2[:, 0:2], 1.0, None, A.add, None, ["w2"], ["w2"])
+            tt(T.co[:, 3:48:8], T.co[:, 2:48:8], T.co[:, 1:48:8], A.add, ["co", "cob", "cob7", "cob8"] + kcoa, ["coc"])
             ts(T.eb[:, 3:515:4], T.ai[:], 256.0, 64.0, A.is_equal, A.mult, ["ai", "eb"], ["e+"])
-            ts(T.eb[:, 523:1035:4], T.ai[:], 256.0, -64.0, A.is_equal, A.mult, ["ai", "eb"], ["e-"])
-            ts(T.sm[:], T.mk0[:], -2.0 ** -10, 2.0 ** -10, A.mult, A.add, ["mk0"], ["sm"])
-            ts(T.tg[:], T.jf[:], Q320, None, A.is_gt, None, ["jf", "Q320"], ["tg"])
-            fill(T.ha[:, 0:3 * CP:3], 0.0, ["ha0"])
-            act(J0, R1, AF.Identity, ["R1"], ["J0"], scale=float(CP), bias=float(-CP))
         if k == 3:
             equant(0)
             equant(1)
-            tt(T.me[:], T.tg[:], T.sm[:], A.mult, ["tg", "sm"], ["me"])
-        if k == 4:
-            equant(2)
-            equant(3)
-            tt(T.ml2[:], T.me[:], T.sm[:], A.subtract, ["me", "sm"], ["ml2"])
-            ts(T.hb[:, 0:3 * CP:3], T.jf[:, 0:CP], J0, 1.0 / PL, A.add, A.mult, ["jf", "J0"], ["hb0"])
-            op("y", lambda: Y.dma_start(T.vt[:], T.v[:]), ["eq3"], ["vt"], sem="ldv", step=16)
-            op("y", lambda: Y.dma_start(T.wq[:].bitcast(dt.uint8), T.wc[:]), [], ["wq"], sem="ldw", step=16, total=32)
-            op("y", lambda: Y.dma_start(T.wp[:], T.ws[:]), [], ["wp"], sem="ldw", step=16, total=32)
-        if k == 5:
-            fill(T.hb[:, 1:3 * CP:3], 1.0, ["hb1"])
         if k == 6:
-            fill(T.fg[:, 32:PE + 33:PE], 0.0, ["fgp"])
+            equant(2)
+        if k == 7:
+            equant(3)
         if k == 8:
             ts(T.dmp[:], T.jm[:], R1, 2048.0, A.is_equal, A.mult, ["jm", "R1"], ["dmp"])
-        if k == 9:
-            for b in (2, 3):
-                quant(T.eq[:, 256 + 128 * b:384 + 128 * b], T.es[:, 256 + 128 * b:384 + 128 * b], T.eb[:, 523 - b:1035 - b], ["e-"], ["eq%d" % (2 + b)])
+            clear(0)
 
-    def lo(k):
-        return T.rr[:, (k - 1) * SL + 31:(k - 1) * SL + 32]
+    def extras_v(k):
+        if k == 4:
+            ts(T.mk0[:], T.jf[:, 0:32], float(C + 16), HH, A.is_ge, A.is_equal, ["jf", "HH"], ["mk0"])
+        if k == 5:
+            tt(T.tg[:], T.tg[:], T.mk0[:], A.mult, ["tg", "mk0"], ["tg"])
+
+    def extras_a(k):
+        if k == 1:
+            act(JZ, R1, AF.Relu, ["R1"], ["JZ"], scale=-2.0, bias=4.0)
+        if k == 2:
+            act(NQ, HH, AF.Identity, ["HH", "R320"], ["NQ"], scale=16.0, bias=R320)
+            act(I0, R1, AF.Identity, ["R1"], ["I0"], scale=-2.0 * FP, bias=2.0 * FP * 17 - F)
+            act(JJ, R1, AF.Identity, ["R1"], ["JJ"], scale=2.0 * JW, bias=2.0 * (C - JW))
+        if k == 3:
+            act(NQ, NQ, AF.Identity, ["NQ"], ["NQ"], scale=-1.0, bias=-0.5)
+            afill(T.ha[:, 0:4 * CP:4], CP, 0.0, [], ["ha0"])
+            afill(T.ha[:, 1:4 * CP:4], CP, 1.0, [], ["ha1"])
+        if k == 4:
+            act(T.tg[:], T.jf[:, 0:32], AF.Sign, ["jf", "NQ"], ["tg"], bias=NQ)
+            act(T.hb[:, UO:UO + 4 * CP:4], T.jf[:, 0:CP], AF.Identity, ["jf", "JJ"], ["hb0"], scale=2.0, bias=JJ)
+            afill(T.hb[:, UO + 2:UO + 4 * CP:4], CP, 2.0 * PL, [], ["hb2"])
+        if k == 5:
+            afill(T.pl[:, 0:31], 31, 4096.0, [], ["pl0"])
+            afill(T.pl[:, 31:33], 2, 0.0, [], ["pl1"])
+            afill(T.fg[:, 65:66], 1, 0.0, [], ["fg0"])
+        if k == 6:
+            act(T.mb[:, 32:64], T.tg[:], AF.Identity, ["tg"], ["mb1"], scale=1024.0)
+            afill(T.dq[:, 0:FP], FP, -BIG, [], ["dqa"])
+            afill(T.dq[:, 3 * FP:4 * FP], FP, BIG, [], ["dqb"])
+        if k == 7:
+            act(T.mk0[:], T.tg[:], AF.Relu, ["tg"], ["mk0"], scale=-1.0)
+        if k == 8:
+            act(T.mb[:, 0:32], T.mk0[:], AF.Identity, ["mk0"], ["mb0"], scale=-1024.0)
+
+    def th(k):
+        return T.th[:, k:k + 1]
+
+    def quant_state(t, i, src, reads):
+        a, b = parts(TA[t])[i]
+        quant(T["tq%d" % t][:, a:b], T["ts%d" % t][:, a:b], src[:, 4 * a:4 * b], reads, ["tq%d%d" % (t, i)])
+
+    def scores(t, i):
+        a, b = parts(TA[t])[i]
+        for w in range(2):
+            mx(2 * i + w, b - a, T.uq2[:, 128 * w:128 * w + 128], T.us2[:, 128 * w:128 * w + 128],
+               T["tq%d" % t][:, a:b], T["ts%d" % t][:, a:b], ["uq2", "us2", "tq%d%d" % (t, i)])
+
+    def relu_z(t, i):
+        a, b = parts(TA[t])[i]
+        if t == 0:
+            act(T.xx[:, a:b], bank(2 * i, b - a), AF.Relu, ["bk%d" % (2 * i)], ["B%d" % i], scale=-1.0)
+        else:
+            act(T.nz[:, a:b], bank(2 * i, b - a), AF.Relu, ["bk%d" % (2 * i)], ["nz%d" % i], scale=-1.0)
+
+    def abs_s(t, i):
+        a, b = parts(TA[t])[i]
+        act(T.ab[:, a:b], bank(2 * i + 1, b - a), AF.Abs, ["bk%d" % (2 * i + 1)], ["ab%d" % i])
+
+    def low(t, i):
+        a, b = parts(TA[t])[i]
+        tt(T.xx[:, a:b], T.mm[:, a:b], T.nz[:, a:b], A.add, ["mm", "nz%d" % i], ["B%d" % i])
+
+    def high(t, i):
+        a, b = parts(TA[t])[i]
+        tt(T.xx[:, C + a:C + b], T.xx[:, a:b], T.ab[:, a:b], A.add, ["B%d" % i, "ab%d" % i], ["HI%d" % i])
+
+    def count1(a, b, col, reads, neg=False):
+        if neg:
+            act(T.junk[:, a:b], T.xx[:, a:b], AF.Sign, reads + ["nt1"], ["j%d" % col, "c%d" % col], bias=NT1, accum_out=T.sc[:, col:col + 1])
+        else:
+            act(T.junk[:, a:b], T.xx[:, a:b], AF.Sign, reads + ["t1"], ["j%d" % col, "c%d" % col], scale=-1.0, bias=T.t1[:, 15:16],
+                accum_out=T.sc[:, col:col + 1])
 
     sent = 0
-    H = C // 2
+    KX = ["B0", "B1", "HI0", "HI1"]
+    KJ = ["j9", "j10", "j11", "j12"]
+    KR = ["r00", "r01", "r10", "r11"]
+    quant_state(0, 0, T.xt, ["xt0"])
+    scores(0, 0)
+    quant_state(0, 1, T.xt, ["xt1"])
+    scores(0, 1)
+    op("y", lambda: Y.dma_start(T.wq[:].bitcast(dt.uint8), T.wc[:]), ["tq01"], ["wq"], sem="ldw", step=16, total=32)
+    op("y", lambda: Y.dma_start(T.wp[:], T.ws[:]), [], ["wp"], sem="ldw", step=16, total=32)
+    relu_z(0, 0)
+    abs_s(0, 0)
+    relu_z(0, 1)
+    abs_s(0, 1)
+    extras(0)
+    high(0, 0)
+    high(0, 1)
+    extras(-1)
+
     for t in range(ROUNDS):
         other = T.cores[rank ^ PARTNER[t]]
         h1, h2, h3 = helpers(core, other, topo)
         tq, tsc, pq, psc = T["tq%d" % t], T["ts%d" % t], T["pq%d" % t], T["ps%d" % t]
-        ao, la, sw = T["ao%d" % t], T["la%d" % t], T["sw%d" % t]
-        ktq, kao, ksw = "tq%d" % t, "ao%d" % t, ["swa%d" % t, "swb%d" % t]
+        ao, la, sw = T["ao%d" % t], T["la%d" % t], T.sw
+        ktq, kao, ksw = ["tq%d0" % t, "tq%d1" % t], "ao%d" % t, ["sw0", "sw1"]
         bulk, lst = T.sem["bulk%d" % t], T.sem["lst%d" % t]
-        if t == 0:
-            quant(tq[:], tsc[:], T.xt[:], ["xt"], [ktq])
-            extras(0)
-        else:
-            quant(tq[:], tsc[:], T.tt[:], ["tt0", "tt1", "tt2", "tt3"], [ktq])
+        ta = TA[t]
 
         eng = topo.engines(core, h1)
         n = len(eng)
@@ -294,8 +377,8 @@ def rank_program(g, core, T, topo):
             trs.append(RemoteDMATransfer(dst_ids=[DstId(rid=rid, pnc=pid)], dma_engine_mask=bits(es), remote_sem=bulk,
                                          src=tq[:, a:a + H].bitcast(dt.uint8), dst=pq[:, a:a + H].bitcast(dt.uint8)))
         rid2, pid2 = topo.addr(h2, core)
-        op("g", lambda: g.remote_dma_fused(trs, local_sem=T.sem.sent), [ktq], [], step=0)
-        op("g", lambda: g.remote_dma(psc[:], tsc[:], bulk, T.sem.sent, pid2, rid2, bits(eng)), [ktq], [], step=0)
+        op("g", lambda: g.remote_dma_fused(trs, local_sem=T.sem.sent), ktq, [], step=0)
+        op("g", lambda: g.remote_dma(psc[:], tsc[:], bulk, T.sem.sent, pid2, rid2, bits(eng)), ktq, [], step=0)
         sent += 3 * n
         oh = helpers(other, core, topo)
         writer["pq"] = ("bulk%d" % t, sum(len(topo.engines(h, core)) for h in oh), {})
@@ -303,171 +386,205 @@ def rank_program(g, core, T, topo):
         writer["la"] = ("lst%d" % t, len(topo.engines(oh[1], core)), {})
         readers["la"] = []
 
-        mx(0, T.uq2[:, 0:128], T.us2[:, 0:128], tq[:], tsc[:], True, True, ["uq2", "us2", ktq])
-        mx(1, T.uq2[:, 128:256], T.us2[:, 128:256], tq[:], tsc[:], True, True, ["uq2", "us2", ktq])
-        B, HI = T.xx[:, 0:C], T.xx[:, C:F]
-        t1 = T.t1[:, 15:16]
-        s0 = T.sc[:, 0:1]
-        if t == 0:
-            act(B, bank(0), AF.Relu, ["bk0"], ["B"], scale=-1.0)
-        else:
-            act(T.nz[:], bank(0), AF.Relu, ["bk0"], ["nz"], scale=-1.0)
-            tt(B, T.mm[:], T.nz[:], A.add, ["mm", "nz"], ["B"])
-        act(T.ab[:], bank(1), AF.Abs, ["bk1"], ["ab"])
-        tt(HI, B, T.ab[:], A.add, ["B", "ab"], ["HI"])
-        if t > 0:
-            act(T.rv[:, 0:F:2], bank(1), AF.Relu, ["bk1"], ["r0"], scale=-1.0)
-        act(T.junk[:, 0:C], B, AF.Sign, ["B", "nt1"], ["j0", "s0"], bias=NT1, accum_out=s0)
-        if t == 0:
-            act(T.rv[:, 0:F:2], bank(1), AF.Relu, ["bk1"], ["r0"], scale=-1.0)
-            ts(T.mk2[:], T.mk[:], s0, None, A.add, None, ["mk", "s0"], ["mk2"])
-
-        thr, kthr = t1, "t1"
-        nb = T.dd[:, 4 * SL + 32:4 * SL + 33]
+        count1(0, ta, 9, ["B0"])
+        count1(C, C + ta, 11, ["HI0"])
+        count1(ta, C, 10, ["B1"])
+        count1(C + ta, F, 12, ["HI1"], neg=True)
+        ts(T.sc[:, 13:14], T.sc[:, 10:11], T.sc[:, 11:12], T.sc[:, 9:10], A.add, A.add, ["c9", "c10", "c11"], ["c13"])
         for k in range(1, 9):
-            sk = T.sc[:, k:k + 1]
-            d = (SHARE if t > 0 else SHARE0).get(k, 0)
+            off = T.of[:, 2 * k - 2:2 * k - 1]
+            thr, kthr = th(k), "th%d" % k
             if k == 1:
-                act(T.junk[:, C + d:F], T.xx[:, C + d:F], AF.Sign, ["HI", kthr], ["j1", "s1"], scale=-1.0, bias=thr, accum_out=sk)
-                act(T.rv[:, 1:F:2], bank(1), AF.Relu, ["bk1"], ["r1"])
-                op("y", lambda: Y.dma_start(T.bd[:], T.xx[0:128:16, 0:C]), ["B", "HI"], ["bd"], sem="deal", step=16, total=32 * (t + 1))
-                op("y", lambda: Y.dma_start(T.rd[:], T.rv[0:128:16, :]), ["r0", "r1"], ["rd"], sem="deal", step=16, total=32 * (t + 1))
-                vsrc, ksrc = T.xx[:, C:C + d], ["HI"]
+                ts(off, T.sc[:, 12:13], T.sc[:, 13:14], J2, A.is_gt, A.add, ["c12", "c13", "J2"], ["of1"])
             else:
-                src, ksrc = (T.xx, ["B", "HI"]) if k < 8 else (T.dv, ["dv0", "dv1"])
-                act(T.junk[:, d:F], src[:, d:F], AF.Sign, ksrc + [kthr], ["j0", "j1", "s%d" % k], scale=-1.0, bias=thr, accum_out=sk)
-                vsrc = src[:, 0:d]
-            if d:
-                ts(T.gl[:, GW - d:GW], vsrc, thr, 2.0, A.is_gt, A.mult, ksrc + [kthr], ["gl"])
-            if k == 3:
-                ts(T.dd[:], T.co[:], lo(2), None, A.mult, None, ["co", "co0", "co1", "co2", "co3", "co4", "rr2"], ["dd", "nb"])
-            if k == 4:
-                ts(nb, lo(2), 2.0 ** -8, lo(3), A.mult, A.subtract, ["rr2", "rr3"], ["nb"])
-            if k in (5, 6):
-                a = C * (k - 5)
-                ts(T.dv[:, a:a + C], T.xx[:, a:a + C], TAU, nb, A.max, A.add, ["B", "HI", "nb"], ["dv%d" % (k - 5)])
-            if k == 7:
+                d = SHARE[k]
+                sk = T.sc[:, k:k + 1]
+                src, ksrc = (T.xx, KX) if k < 7 else (T.dv, ["dv0", "dv1"])
+                act(T.junk[:, d:F], src[:, d:F], AF.Sign, ksrc + [kthr], KJ + ["s%d" % k], scale=-1.0, bias=thr, accum_out=sk)
+                if k == 2:
+                    cp(T.pb[:, 0:1], thr, [kthr], ["pb0"])
+                if k == 3:
+                    ts(T.pb[:, 1:2], thr, KAP, None, A.mult, None, [kthr, "KAP"], ["pb1"])
+                ts(T.gl[:, 0:d], src[:, 0:d], thr, None, A.is_gt, None, ksrc[:2] + [kthr], ["gl"])
+                o = 8 * (k - 3)
+                if k == 2:
+                    ts(T.sc[:, 14:15], K2, T.pb[:, 0:1], None, A.mult, None, ["K2", "pb0"], ["sc2"])
+                elif k == 3:
+                    ts(T.dd[:], T.co[:], T.pb[:, 1:2], None, A.mult, None, kco + ["pb1"], ["ddu"] + ["dd%d" % j for j in range(3, 9)])
+                elif k == 6:
+                    ts(T.dd[:, o + 2:o + 4], T.dd[:, o + 2:o + 4], thr, th(4), A.add, A.subtract, ["dd6", kthr, "th4"], ["dd6"])
+                else:
+                    ts(T.dd[:, o + 2:o + 4], T.dd[:, o + 2:o + 4], thr, None, A.add, None, ["dd%d" % k, kthr], ["dd%d" % k])
+                if t == 0:
+                    extras_v(k)
+                scan(T.mo[:, 0:d], T.gl[:, 0:d], T.gl[:, 0:d], float(-d), A.add, A.add, ["gl"], ["mo"])
+                if k == 3:
+                    ts(T.dd[:, 2:4], T.dd[:, 2:4], thr, None, A.add, None, ["dd3", kthr], ["dd3"])
+                ts(off, T.mo[:, d - 1:d], sk, J2 if k == 2 else JZ, A.is_gt, A.add, ["mo", "s%d" % k, "J2", "JZ"], ["of%d" % k])
+            if t == 0:
+                extras_a(k)
+            nxt, kn = th(k + 1), ["j16", "th%d" % (k + 1)]
+            if k == 1:
+                act(T.j16[:], T.w1[:].indirect(off), AF.Identity, ["w11", "w10", "of1"], kn, accum_out=nxt)
+            elif k == 2:
+                act(T.j16[:], T.w2[:].indirect(off), AF.Identity, ["w2", "of2", "sc2"], kn, scale=T.sc[:, 14:15], accum_out=nxt)
+            else:
+                act(T.j16[:], T.dd[:, o:o + 4].indirect(off), AF.Identity, ["dd%d" % k, "of%d" % k], kn, accum_out=nxt)
+            if k in (1, 2):
+                for i, (a, b) in enumerate(parts(ta)):
+                    out, kb = T.rv[:, 2 * a + k - 1:2 * b:2], "bk%d" % (2 * i + 1)
+                    if k == 1:
+                        ts(out, bank(2 * i + 1, b - a), -1.0, 0.0, A.mult, A.max, [kb], ["r0%d" % i])
+                    else:
+                        ts(out, bank(2 * i + 1, b - a), 0.0, None, A.max, None, [kb], ["r1%d" % i])
+            if k == 1:
+                op("y", lambda: Y.dma_start(T.bd[:], T.xx[0:128:16, 0:C]), ["B0", "B1"], ["bd"], sem="deal", step=16, total=32 * (t + 1))
+            if k == 2:
+                op("y", lambda: Y.dma_start(T.rd[:], T.rv[0:128:16, :]), KR, ["rd"], sem="deal", step=16, total=32 * (t + 1))
+                if t == 0:
+                    op("y", lambda: Y.dma_start(T.vt[:], T.v[:]), ["rd"], ["vt"], sem="ldv", step=16)
+            if k in (4, 5):
+                a = C * (k - 4)
+                ts(T.dv[:, a:a + C], T.xx[:, a:a + C], TAU, th(4), A.max, A.subtract, KX + ["th4"], ["dv%d" % (k - 4)])
+            if k == 6:
                 tt(T.cd[:, 0:FP:2], T.bd[:], T.rd[:, 0:FP:2], A.add, ["bd", "rd"], ["cd0"])
                 tt(T.cd[:, 1:FP:2], T.bd[:], T.rd[:, 1:FP:2], A.add, ["bd", "rd"], ["cd1"])
-            if k == 8:
-                ts(T.dvd[:], T.cd[:], TAU, nb, A.max, A.add, ["cd0", "cd1", "nb"], ["dvd"])
+            if k == 7:
+                ts(T.dq[:, 2 * FP:3 * FP], T.cd[:], TAU, th(4), A.max, A.subtract, ["cd0", "cd1", "th4"], ["dq2"])
             if t == 0:
                 extras(k)
-            if d:
-                mo = T.mo1 if k == 1 else T.mo
-                scan(mo[:, GW - d:GW + 32], T.gl[:, GW - d:GW + 32], T.md[:, GW - d:GW + 32], s0 if k == 1 else 0.0, A.add, A.add,
-                     ["gl", "glt", "md0", "md1", "md2"] + (["s0"] if k == 1 else []), ["mo"])
-                mask, kmask = mo[:, GW:GW + 32], "mo"
-            elif k == 1:
-                mask, kmask = T.mk2[:], "mk2"
-            else:
-                mask, kmask = T.mk[:], "mk"
-            ts(T.fl[:], mask, sk, thr, A.is_gt, A.mult, [kmask, "s%d" % k, kthr], ["fl"])
-            op("v", lambda: V.transpose(T.ft[:, 0:32], T.fl[:]), ["fl"], ["ft"])
-            w = 35 if k == 7 else 33
-            if k <= 2:
-                d1, o1, kd = T.d12[:, (k - 1) * SL:(k - 1) * SL + w], A.mult, ["d12"]
-            else:
-                d1, o1, kd = T.dd[:, (k - 3) * SL:(k - 3) * SL + w], A.add, ["dd"] + (["nb"] if k == 7 else [])
-            if k == 1:
-                init, ki = TAU, []
-            elif k == 8:
-                init, ki = T.rr[:, 6 * SL + 33:6 * SL + 34], ["rr7"]
-            else:
-                init, ki = lo(k - 1), ["rr%d" % (k - 1)]
-            o = (k - 1) * SL
-            scan(T.rr[:, o:o + w], T.ft[:, 0:w], d1, init, A.max, o1, ["ft"] + kd + ki, ["rr%d" % k])
-            thr, kthr = T.rr[:, o + w - 1:o + w], "rr%d" % k
+            if k == 7:
+                ts(T.dq[:, FP:2 * FP], T.dq[:, 2 * FP:3 * FP], T.dd[:, 44:45], None, A.subtract, None, ["dq2", "ddu"], ["dq1"])
 
-        act(T.jk2[:, 0:FP], T.dvd[:], AF.Sign, ["dvd", "rr8"], ["jk0", "s9"], scale=-1.0, bias=lo(8), accum_out=T.sc[:, 9:10])
-        act(T.jk2[:, FP:2 * FP], T.dvd[:], AF.Sign, ["dvd", "rr8"], ["jk1", "s10"], scale=-1.0, bias=thr, accum_out=T.sc[:, 10:11])
-        ts(T.fg[:, 33:PW], T.dvd[:], lo(8), 1.0 / PL, A.is_lt, A.mult, ["dvd", "rr8"], ["fg0"])
-        ts(T.fg[:, PE + 33:PE + PW], T.dvd[:], thr, 1.0 / PL, A.is_lt, A.mult, ["dvd", "rr8"], ["fg1"])
-        ts(T.fl2[:, 0:32], T.ml2[:], T.sc[:, 9:10], None, A.mult, None, ["ml2", "s9"], ["fl20"])
-        ts(T.fl2[:, 32:64], T.me[:], T.sc[:, 10:11], None, A.mult, None, ["me", "s10"], ["fl21"])
-        op("v", lambda: V.transpose(T.fg[:, 0:32], T.fl2[:, 0:32]), ["fl20"], ["fa0"])
-        op("v", lambda: V.transpose(T.fg[:, PE:PE + 32], T.fl2[:, 32:64]), ["fl21"], ["fa1"])
-        kc = ["cs", "cs0", "fgp"]
-        scan(T.kt[:, 0:PW], T.fg[:, 0:PW], T.cs[:, 0:PW], 0.0, A.add, A.add, ["fg0", "fa0"] + kc, ["kt"])
-        scan(T.ke[:, 0:PW], T.fg[:, PE:PE + PW], T.cs[:, 0:PW], 0.0, A.add, A.add, ["fg1", "fa1"] + kc, ["ke"])
-        tt(T.kk[:, 0:FP + 1], T.kt[:, 32:PW], T.ke[:, 32:PW], A.min, ["kt", "ke"], ["kk"])
-        tt(T.hb[:, 2:3 * CP:3], T.kt[:, 32:PW - 1:2], T.ke[:, 32:PW - 1:2], A.min, ["kt", "ke"], ["hb2"])
-        tt(T.ha[:, 1:3 * CP:3], T.kk[:, 2:FP + 1:2], T.kk[:, 1:FP:2], A.is_equal, ["kk"], ["ha1"])
-        tt(T.ha[:, 2:3 * CP:3], T.kk[:, 1:FP:2], T.kk[:, 0:FP:2], A.is_equal, ["kk"], ["ha2"])
-        scan(T.hs[:], T.ha[:], T.hb[:], 0.0, A.mult, A.add, ["ha0", "ha1", "ha2", "hb0", "hb1", "hb2"], ["hs"])
-        ts(T.so[:], T.hs[:, 2:3 * CP:3], float(PL), None, A.mult, None, ["hs"], ["so"])
+        LO = th(9)
+        act(T.jk2[:, 0:2 * FP], T.dq[:, 0:2 * FP], AF.Sign, ["dqa", "dq1", "th9"], ["jk0", "s0"], scale=-1.0, bias=LO, accum_out=T.sc[:, 0:1])
+        act(T.jk2[:, 2 * FP:4 * FP], T.dq[:, 2 * FP:4 * FP], AF.Sign, ["dqb", "dq2", "th9"], ["jk1", "s1"], scale=-1.0, bias=LO, accum_out=T.sc[:, 1:2])
+        ts(T.fg[:, 66:66 + 2 * FP], T.dq[:, FP:3 * FP], LO, 2.0, A.is_lt, A.mult, ["dq1", "dq2", "th9"], ["fgf"])
+        lt = T.fg[:, 66 + FP:66 + 2 * FP]
+        if t == 0:
+            clear(1)
+        scan(T.pl[:, 33:33 + FP], lt, lt, 0.0, A.add, A.max, ["fgf"], ["pl2"])
+        ts(T.fl[:], T.mb[:], T.sc[:, 1:2], T.sc[:, 0:1], A.max, A.min, ["mb0", "mb1", "s0", "s1"], ["fl"])
+        op("v", lambda: V.transpose(T.fg[:, 1:65], T.fl[:]), ["fl"], ["fgt"])
+        scan(T.hb[:, 1:2 * (33 + FP):2], T.fg[:, 33:66 + FP], T.pl[:], I0, A.add, A.min, ["fgt", "fg0", "fgf", "I0", "pl0", "pl1", "pl2"], ["U"])
+        op("v", lambda: V.tensor_reduce(T.sc[:, 15:16], T.fg[:, 0:33], AxisListType.X, A.add, negate=True), ["fgt", "I0"], ["L0"])
+        u0, u1, u2 = (T.hb[:, UO + 3 + 2 * j:UO + 2 * j + 4 * CP:4] for j in range(3))
+        tt(T.ha[:, 2:4 * CP:4], u2, u1, A.is_equal, ["U"], ["ha2"])
+        tt(T.ha[:, 3:4 * CP:4], u1, u0, A.is_equal, ["U"], ["ha3"])
+        scan(T.hs[:], T.ha[:], T.hb[:, UO:UO + 4 * CP], 0.0, A.mult, A.add, ["ha0", "ha1", "ha2", "ha3", "hb0", "hb2", "U"], ["hs"])
+        ts(T.so[:], T.hs[:, 3:4 * CP:4], T.sc[:, 15:16], 0.5, A.add, A.mult, ["hs", "L0"], ["so"])
         cp(sw[:, 0:SW].indirect(T.so[:]), T.jv[:], ["so", "jv"], ksw)
         scan(T.fi[:], sw[:, 0:C], sw[:, PL:PL + C], -256.0, A.max, A.max, ksw, ["fi"])
         scan(T.gf[:], T.dmp[:], T.fi[:], 0.0, A.add, A.min, ["dmp", "fi"], ["gf"])
         ts(ao[:], T.gf[:, 15:C:16], float(H), None, A.add, None, ["gf"], [kao])
         op("g", lambda: g.remote_dma(la[:], ao[:], lst, T.sem.sent, pid2, rid2, bits(eng)), [kao], [], step=0)
 
-        for b in (0, 1):
-            unit(2 + b, b, tq, tsc, True, [ktq])
         for b in range(4):
-            unit(4 + b, b, pq, psc, True, ["pq"])
-        for b in (0, 1):
-            act(T.dn[:, C * b:C * b + C], bank(2 + b), AF.Copy, ["bk%d" % (2 + b)], ["dn%d" % b])
+            unit(4 + b, b, tq, tsc, ktq)
         for b in range(4):
-            act(T.dp[:, C * b:C * b + C], bank(4 + b), AF.Identity, ["bk%d" % (4 + b)], ["dp%d" % b], scale=1.0 / 64)
+            unit(b, b, pq, psc, ["pq"])
+        for b in range(4):
+            act(T.dn[:, C * b:C * b + C], bank(4 + b), AF.Identity, ["bk%d" % (4 + b)], ["dn%d" % b], scale=1.0 / 64 if b % 2 else 1.0)
+        for b in range(4):
+            act(T.dp[:, C * b:C * b + C], bank(b), AF.Identity, ["bk%d" % b], ["dp%d" % b], scale=1.0 / 64)
 
-        act(T.bg[:], T.xx[:, 0:C].indirect(ao[:]), AF.Copy, ["B", kao], ["bg"])
+        act(T.bg[:], T.xx[:, 0:C].indirect(ao[:]), AF.Copy, ["B0", "B1", kao], ["bg"])
+        for b in (1, 3):
+            act(T.hz[:, H * (b - 1):H * (b - 1) + C], T.dn[:, C * b:C * b + C].indirect(ao[:]), AF.Copy, ["dn%d" % b, kao], ["hz%d" % b])
         ts(T.bt[:], sw[:, 0:C], -256.0, 0.5, A.is_equal, A.mult, ksw, ["bt"])
-        if t == 0:
-            extras(9)
         tt(T.kh[:], T.fi[:], T.bt[:], A.add, ["fi", "bt"], ["kh"])
+        if t + 1 < ROUNDS:
+            clear(0)
         scan(T.gk[:], T.dmp[:], T.kh[:], 0.0, A.add, A.min, ["dmp", "kh"], ["gk"])
-        if t == 1:
-            quant(T.vq[:], T.vs[:], T.vt[:], ["vt"], ["vq"])
+        if t + 1 < ROUNDS:
+            clear(1)
         if t == ROUNDS - 1:
             ts(T.kf[:], T.kh[:], 2.0, float(C), A.mult, A.add, ["kh"], ["kf"])
         ts(T.ko[:], T.gk[:, 15:C:16], 2.0, float(C), A.mult, A.add, ["gk"], ["ko"])
-        tt(T.mm[:], T.rv[:].indirect(T.ko[:]), T.bg[:], A.add, ["r0", "r1", "ko", "bg"], ["mm"])
+        if t == 1:
+            quant(T.vq[:], T.vs[:], T.vt[:], ["vt"], ["vq"])
+        tt(T.mm[:], T.rv[:].indirect(T.ko[:]), T.bg[:], A.add, KR + ["ko", "bg"], ["mm"])
         if t == ROUNDS - 1:
             op("y", lambda: Y.dma_start(T.kl[:], T.kf[0:128:16, :]), ["kf"], [], sem="stk", step=16)
             op("y", lambda: Y.dma_start(T.ml[:], T.mm[0:128:16, :]), ["mm"], [], sem="stk", step=16)
-        for b in (2, 3):
-            unit(2 * b, b, tq, tsc, False, [ktq])
-            unit(2 * b + 1, 2 + b, tq, tsc, False, [ktq])
 
-        for b in (0, 1):
-            cp(T.zt[:, b:4 * C:4], T.dp[:, C * b:C * b + C].indirect(la[:]), ["dp%d" % b, "la"], ["zt%d" % b])
-        for b in (2, 3):
-            act(T.zt[:, b:4 * C:4], T.dp[:, C * b:C * b + C].indirect(la[:]), AF.Copy, ["dp%d" % b, "la"], ["zt%d" % b])
-        quant(T.zq[:], T.zs[:], T.zt[:], ["zt0", "zt1", "zt2", "zt3"], ["zq"])
-        if t + 1 < ROUNDS:
-            clear(t + 1)
-        for b, bk in ((0, 0), (2, 4), (2, 5), (1, 1), (3, 6), (3, 7)):
-            mx(bk, T.wq[:, 128 * b:128 * b + 128], T.wp[:, 128 * b:128 * b + 128], T.zq[:], T.zs[:], b < 2, True, ["wq", "wp", "zq"])
-
-        def child(b, s):
-            out, wr = T.tw[:, F * b + s:F * b + F:2], ["tw%d%d" % (b, s)]
-            if b < 2:
-                tt(out, T.dn[:, C * b:C * b + C], bank(b), A.add if s == 0 else A.subtract, ["dn%d" % b, "bk%d" % b], wr)
+        def gather(e, b, i):
+            lo, hi = parts(ZA)[i]
+            out, win = T.zt[:, 4 * lo + b:4 * hi:4], T.dp[:, C * b:C * b + C].indirect(la[:, lo // 16:hi // 16])
+            if e == "v":
+                cp(out, win, ["dp%d" % b, "la"], ["zt%d%d" % (b, i)])
             else:
-                act(out, bank(2 * b + s), AF.Identity, ["bk%d" % (2 * b + s)], wr, scale=2.0 ** -6 if s == 0 else -2.0 ** -6)
+                act(out, win, AF.Copy, ["dp%d" % b, "la"], ["zt%d%d" % (b, i)])
 
-        def pick(b):
-            out, win = T.tt[:, b:4 * C:4], T.tw[:, F * b:F * b + F].indirect(T.ko[:])
-            rd, wr = ["tw%d0" % b, "tw%d1" % b, "ko"], ["tt%d" % b]
-            if b < 2:
-                ts(out, win, 2.0 ** -6, None, A.mult, None, rd, wr)
+        def products(i):
+            lo, hi = parts(ZA)[i]
+            quant(T.zq[:, lo:hi], T.zs[:, lo:hi], T.zt[:, 4 * lo:4 * hi], ["zt%d%d" % (b, i) for b in range(4)], ["zq%d" % i])
+            for b in (1, 0, 3, 2):
+                mx(2 * b + i, hi - lo, T.wq[:, 128 * b:128 * b + 128], T.wp[:, 128 * b:128 * b + 128], T.zq[:, lo:hi], T.zs[:, lo:hi],
+                   ["wq", "wp", "zq%d" % i])
+
+        def child(b, i):
+            lo, hi = parts(ZA)[i]
+            bk, kb, o = bank(2 * b + i, hi - lo), "bk%d" % (2 * b + i), F * (b // 2)
+            for s in range(2):
+                wr = ["ch%d%d%d" % (b, i, s)]
+                if b % 2 == 0:
+                    tt(T.tw[:, o + 2 * lo + s:o + 2 * hi:2], T.dn[:, C * b + lo:C * b + hi], bk, A.add if s == 0 else A.subtract, ["dn%d" % b, kb], wr)
+                else:
+                    act(T.rw[:, o + 2 * lo + s:o + 2 * hi:2], bk, AF.Identity, [kb], wr, scale=2.0 ** -6 if s == 0 else -2.0 ** -6)
+
+        def pick(b, i):
+            lo, hi = parts(TA[t + 1])[i]
+            out, l, o = T.tt[:, 4 * lo + b:4 * hi:4], T.ko[:, lo // 16:hi // 16], F * (b // 2)
+            rd, wr = ["ch%d%d%d" % (b, j, s) for j in range(2) for s in range(2)] + ["ko"], ["tt%d%d" % (b, i)]
+            if b % 2 == 0:
+                act(out, T.tw[:, o:o + F].indirect(l), AF.Identity, rd, wr, scale=2.0 ** -6)
             else:
-                act(out, win, AF.Copy, rd, wr)
+                z = H * (b - 1)
+                tt(out, T.rw[:, o:o + F].indirect(l), T.hz[:, z + lo:z + hi], A.add, rd + ["hz%d" % b], wr)
 
-        for b in range(4):
-            child(b, 0)
-            child(b, 1)
-            pick(b)
+        for e, b, i in (("v", 0, 0), ("a", 2, 0), ("v", 1, 0), ("a", 3, 0), ("v", 0, 1), ("a", 2, 1), ("a", 3, 1)):
+            gather(e, b, i)
+        products(0)
+        gather("v", 1, 1)
+        products(1)
+        for i in range(2):
+            for b in (1, 0, 3, 2):
+                child(b, i)
+        for b in (1, 0, 3, 2):
+            pick(b, 0)
+        u = t + 1
+        quant_state(u, 0, T.tt, ["tt%d0" % b for b in range(4)])
+        for b in (1, 0, 3, 2):
+            pick(b, 1)
+        if u < ROUNDS:
+            scores(u, 0)
+            relu_z(u, 0)
+            abs_s(u, 0)
+            quant_state(u, 1, T.tt, ["tt%d1" % b for b in range(4)])
+            scores(u, 1)
+            relu_z(u, 1)
+            abs_s(u, 1)
+            low(u, 0)
+            high(u, 0)
+            low(u, 1)
+            high(u, 1)
 
-    tq, tsc, ktq = T["tq%d" % ROUNDS], T["ts%d" % ROUNDS], "tq%d" % ROUNDS
-    quant(tq[:], tsc[:], T.tt[:], ["tt0", "tt1", "tt2", "tt3"], [ktq])
-    mx(0, T.vq[:], T.vs[:], tq[:], tsc[:], True, True, ["vq", ktq])
-    op("y", lambda: Y.dma_start(T.oc[:], tq[:].bitcast(dt.uint8)), [ktq], [], sem="sto", step=16)
-    for k in range(4):
-        op("y", lambda: Y.dma_start(T.osc[4 * k:4 * k + 4, :], tsc[32 * k:32 * k + 4, :]), [ktq], [], sem="sto", step=16)
-    act(T.yo[:], bank(0), AF.Copy, ["bk0"], ["yo"])
-    op("a", lambda: S.dma_start(T.y[:], T.yo[:]), ["yo"], [], sem="sty", step=16)
+    tq, tsc = T["tq%d" % ROUNDS], T["ts%d" % ROUNDS]
+    for i, (a, b) in enumerate(parts(TA[ROUNDS])):
+        ktq = "tq%d%d" % (ROUNDS, i)
+        if i == 1:
+            quant_state(ROUNDS, 1, T.tt, ["tt%d1" % j for j in range(4)])
+        mx(i, b - a, T.vq[:], T.vs[:], tq[:, a:b], tsc[:, a:b], ["vq", ktq])
+        op("y", lambda: Y.dma_start(T.oc[:, 4 * a:4 * b], tq[:, a:b].bitcast(dt.uint8)), [ktq], [], sem="sto", step=16)
+        if i == 0:
+            act(T.yo[:, a:b], bank(i, b - a), AF.Copy, ["bk0"], ["yo0"])
+            op("a", lambda: S.dma_start(T.y[:, a:b], T.yo[:, a:b]), ["yo0"], [], sem="sty", step=16)
+        else:
+            for k in range(4):
+                op("y", lambda: Y.dma_start(T.osc[4 * k:4 * k + 4, :], tsc[32 * k:32 * k + 4, :]), [ktq], [], sem="sto", step=16)
+            cp(T.yo[:, a:b], bank(i, b - a), ["bk1"], ["yo1"])
+            op("a", lambda: S.dma_start(T.y[:, a:b], T.yo[:, a:b]), ["yo1"], [], sem="sty", step=16)
     g.wait_ge(T.sem.sent, sent)
     for s in ("sg", "sv", "sp", "sa", "stk", "sto", "sty", "deal"):
         g.wait_ge(T.sem[s], count[s])

from concourse.bass import DstId, RemoteDMATransfer
from concourse.mybir import dt, AluOpType, ActivationFunctionType, AxisListType

C = 320
F = 2 * C
H = C // 2
ROUNDS = 3
PARTNER = [1, 2, 4]
TAU = 2.0 ** -100
BIG = 2.0 ** 99
GW = 224
SHARE = {2: 176, 3: 176, 4: 224, 5: 224, 6: 224, 7: 224, 8: 224}
CP = C // 16
FP = 2 * CP
PL = 512
JW = 2 * C + 64
SW = PL + 2 * C + 16 * JW
UO = 62
ZA = 160
TA = [160, 192, 192, 192]
Q4 = "float8_e4m3fn_x4"

SCRATCH = {}
for _dt, _list in (
    ("bfloat16", (("xt", 4 * C), ("tt", 4 * C), ("ut", 512), ("vt", 512), ("eb", 520), ("zt", 4 * C), ("dp", 4 * C), ("dn", 4 * C),
                  ("tw", 2 * F), ("hz", 2 * C), ("junk", F), ("jk2", 4 * FP), ("dmp", C), ("jv", C), ("jm", C), ("fi", C), ("gf", C), ("bt", C),
                  ("gl", GW), ("mo", GW), ("pb", 2), ("sw", SW))),
    ("float32", (("pf", 16), ("jf", 64), ("f1", 16), ("f2", 16), ("fh", 16), ("t1", 16), ("t2", 16), ("t3", 16), ("tl", 16), ("k16", 16),
                 ("z16", 16), ("mk0", 32), ("tg", 32), ("w1", 32), ("w2", 32), ("co", 48), ("dd", 48), ("th", 16), ("sc", 16), ("j16", 16),
                 ("nz", C), ("ab", C), ("rv", F), ("xx", F), ("dv", F), ("mm", C), ("bg", C), ("rw", 2 * F),
                 ("bd", CP), ("rd", FP), ("cd", FP), ("dq", 4 * FP), ("mb", 64), ("fl", 64), ("fg", 66 + 2 * FP), ("pl", 33 + FP),
                 ("ha", 4 * CP), ("hb", UO + 4 * CP + 4), ("hs", 4 * CP),
                 ("kh", C), ("gk", C), ("kf", C), ("yo", C))),
    ("int32", (("pi", 8), ("ui", 16), ("ai", 128))),
    ("uint16", (("uo", 16), ("of", 16), ("so", 20), ("ko", 20), ("ao0", 20), ("ao1", 20), ("ao2", 20), ("la0", 20), ("la1", 20), ("la2", 20))),
    (Q4, (("uq", 128), ("uq2", 256), ("vq", 128), ("wq", 512), ("eq", 512), ("zq", C),
          ("tq0", C), ("tq1", C), ("tq2", C), ("tq3", C), ("pq0", C), ("pq1", C), ("pq2", C))),
    ("uint8", (("us", 128), ("us2", 256), ("vs", 128), ("wp", 512), ("es", 512), ("zs", C),
               ("ts0", C), ("ts1", C), ("ts2", C), ("ts3", C), ("ps0", C), ("ps1", C), ("ps2", C))),
):
    for _name, _n in _list:
        SCRATCH[_name] = ("sbuf", [128, _n], _dt)
for _b in range(8):
    SCRATCH["bk%d" % _b] = ("psum", [128, 512], "float32")

SEMAPHORES = (["sv", "sa", "sp", "sg", "sent", "ldu", "ldxa", "ldxb", "ldv", "ldw", "stk", "sto", "sty", "deal"]
              + ["bulk%d" % t for t in range(ROUNDS)] + ["lst%d" % t for t in range(ROUNDS)])

A = AluOpType
AF = ActivationFunctionType


def bits(engines):
    m = 0
    for e in engines:
        m |= 1 << e
    return m


def helpers(me, other, topo):
    ok = [c for c in topo.cores_of(me) if c != me and topo.may_write(c, other)]
    near = [c for c in ok if topo.die(c) == topo.die(me)]
    far = [c for c in ok if topo.die(c) != topo.die(me)]
    return near[0], near[1], far[0]


def helper_program(g, core, T, topo):
    sent = 0
    for t in range(ROUNDS):
        for r, me in enumerate(T.cores):
            other = T.cores[r ^ PARTNER[t]]
            h1, h2, h3 = helpers(me, other, topo)
            if core not in (h1, h2, h3):
                continue
            rid, pid = topo.addr(other, core)
            mask = topo.mask(core, other)
            n_out = len(topo.engines(core, other))
            n_in = len(topo.engines(me, core))
            bulk, lst = T.sem["bulk%d" % t], T.sem["lst%d" % t]
            if core == h2:
                g.wait_ge(bulk, n_in)
                v = T["ps%d" % t][:]
                g.remote_dma(v, v, bulk, T.sem.sent, pid, rid, mask)
                g.wait_ge(lst, n_in)
                v = T["la%d" % t][:]
                g.remote_dma(v, v, lst, T.sem.sent, pid, rid, mask)
                sent += 2 * n_out
            else:
                a = 0 if core == h1 else H
                g.wait_ge(bulk, n_in // 2)
                g.remote_dma(T["pq%d" % t][:, a:a + H].bitcast(dt.uint8), T["pq%d" % t][:, a:a + H].bitcast(dt.uint8),
                             bulk, T.sem.sent, pid, rid, mask)
                sent += n_out
    if sent:
        g.wait_ge(T.sem.sent, sent)


def rank_program(g, core, T, topo):
    rank = T.rank_of(core)
    if rank is None:
        helper_program(g, core, T, topo)
        return

    V, S, P, Y = g.vector, g.scalar, g.tensor, g.sync
    queue = {"v": V, "a": S, "p": P, "g": g, "y": Y}
    own = {"v": "sv", "a": "sa", "p": "sp", "g": "sg"}
    count = {}
    known = {e: {} for e in queue}
    writer, readers = {}, {}

    def need(e, ev):
        sem, val, clock = ev
        if e == "p" and sem == "sp":
            return
        if known[e].get(sem, 0) < val:
            queue[e].wait_ge(T.sem[sem], val)
            known[e][sem] = val
        for s, n in clock.items():
            if known[e].get(s, 0) < n:
                known[e][s] = n

    def op(e, call, reads, writes, sem=None, step=1, total=None):
        evs = [writer[k] for k in reads if k in writer]
        for k in writes:
            if k in writer:
                evs.append(writer[k])
            evs += readers.get(k, [])
        top = {}
        for ev in evs:
            if ev[0] not in top or top[ev[0]][1] < ev[1]:
                top[ev[0]] = ev
        evs = list(top.values())
        for ev in evs:
            if not any(o is not ev and o[2].get(ev[0], 0) >= ev[1] for o in evs):
                need(e, ev)
        ins = call()
        if step == 0:
            return
        s = sem or own[e]
        ins.then_inc(T.sem[s], step)
        count[s] = count.get(s, 0) + step
        ev = (s, total or count[s], dict(known[e]))
        for k in reads:
            readers.setdefault(k, []).append(ev)
        for k in writes:
            writer[k] = ev
            readers[k] = []

    def ts(out, in0, s1, s2, o0, o1, reads, writes):
        if o1 is None:
            op("v", lambda: V.tensor_scalar(out, in0, s1, None, o0), reads, writes)
        else:
            op("v", lambda: V.tensor_scalar(out, in0, s1, s2, o0, o1), reads, writes)

    def tt(out, in0, in1, o, reads, writes):
        op("v", lambda: V.tensor_tensor(out, in0, in1, o), reads, writes)

    def scan(out, d0, d1, init, o0, o1, reads, writes):
        op("v", lambda: V.tensor_tensor_scan(out, d0, d1, init, o0, o1), reads, writes)

    def fill(ap, val, writes):
        op("v", lambda: V.memset(ap, val), [], writes)

    def cp(out, in_, reads, writes):
        op("v", lambda: V.tensor_copy(out, in_), reads, writes)

    def act(out, in_, f, reads, writes, **kw):
        op("a", lambda: S.activation(out, in_, f, **kw), reads, writes)

    def afill(ap, n, val, reads, writes):
        act(ap, T.jf[:, 0:n], AF.Identity, ["jf"] + reads, writes, scale=0.0, bias=val)

    def iota(out, pattern, base, cm, writes):
        op("g", lambda: g.iota(out, pattern, base, cm, allow_small_or_imprecise_dtypes=True), [], writes)

    def quant(q, s, t, reads, writes):
        op("v", lambda: V.quantize_mx(q, s, t), reads, writes)

    def bank(b, n=C):
        return T["bk%d" % b][:, 0:n]

    def mx(b, n, lq, ls, rq, rs, reads):
        op("p", lambda: P.matmul_mx(bank(b, n), lq, ls, rq, rs, True, True), reads, ["bk%d" % b])

    def unit(bk, e, q, s, reads):
        mx(bk, C, T.eq[:, 128 * e:128 * e + 128], T.es[:, 128 * e:128 * e + 128], q[:], s[:], ["eq%d" % e] + reads)

    def parts(a):
        return ((0, a), (a, C))

    xa = 4 * TA[0]
    op("y", lambda: Y.dma_start(T.ut[:], T.u[:]), [], ["ut"], sem="ldu", step=16)
    op("a", lambda: S.dma_start(T.xt[:, 0:xa], T.x[:, 0:xa]), [], ["xt0"], sem="ldxa", step=16)
    op("y", lambda: Y.dma_start(T.xt[:, xa:4 * C], T.x[:, xa:4 * C]), [], ["xt1"], sem="ldxb", step=16)

    op("g", lambda: g.iota(T.pi[:, 0:1], [[0, 1]], 0, 1), [], ["pi0"])
    iota(T.jf[:], [[1, 64]], C, 0, ["jf"])
    op("g", lambda: g.iota(T.ui[:], [[-1, 2], [16, 8]], 1, 0), [], ["ui"])
    op("g", lambda: g.iota(T.ai[:], [[1, 128]], 256, -1), [], ["ai"])
    iota(T.jm[:], [[0, CP], [1, 16]], 1, 0, ["jm"])
    iota(T.jv[:], [[1, CP], [CP, 16]], -H, 0, ["jv"])

    R1, R320, HH, NQ, NT1, J2, JZ, C3, RM, KAP, JJ = (T.pf[:, i:i + 1] for i in range(11))
    I0 = T.fg[:, 0:1]
    P2, K2 = T.t2[:, 15:16], T.t3[:, 15:16]
    fill(T.k16[:], 4096.0, ["k16"])
    fill(T.z16[:], 0.0, ["z16"])
    fill(T.co[:], 0.0, ["co"])
    fill(T.w1[:], 0.0, ["w1"])
    ts(T.pi[:, 1:2], T.pi[:, 0:1], 15, None, A.bitwise_and, None, ["pi0"], ["pi1"])
    ts(T.pi[:, 2:3], T.pi[:, 0:1], 4, 1, A.logical_shift_right, A.bitwise_and, ["pi0"], ["pi2"])
    scan(T.tl[:], T.k16[:], T.z16[:], TAU, A.mult, A.add, ["k16", "z16"], ["tl"])
    ts(R1, T.pi[:, 1:2], 1.0, None, A.add, None, ["pi1"], ["R1"])
    ts(R320, T.pi[:, 1:2], float(C), None, A.add, None, ["pi1"], ["R320"])
    cp(HH, T.pi[:, 2:3], ["pi2"], ["HH"])
    fill(T.w2[:], 0.0, ["w2"])
    ts(T.f2[:], T.jf[:, 0:16], R320, 1.0, A.is_le, A.add, ["jf", "R320"], ["f2"])
    cp(T.uo[:], T.ui[:], ["ui"], ["uo"])
    fill(T.j16[:], 2.0, ["j16"])
    ts(T.f1[:], T.f2[:], 4095.0, -4094.0, A.mult, A.add, ["f2"], ["f1"])
    scan(T.t2[:], T.f2[:], T.z16[:], 1.0, A.mult, A.add, ["f2", "z16"], ["t2"])
    scan(T.w2[:, 1:32:2], T.j16[:], T.z16[:], 0.5, A.mult, A.add, ["j16", "z16", "w2"], ["w2"])
    scan(T.t1[:], T.f1[:], T.z16[:], TAU, A.mult, A.add, ["f1", "z16"], ["t1"])
    ts(T.w1[:, 1:32:2], T.tl[:], P2, None, A.mult, None, ["tl", "t2", "w1"], ["w11"])

    for k in range(3, 9):
        afill(T.co[:, 8 * k - 23:8 * k - 22], 1, 2.0 ** (8 - 4 * k) if k < 8 else 2.0 ** -23, ["co"], ["coa%d" % k])
    afill(T.co[:, 44:45], 1, 2.0 ** -24, ["co"], ["cod"])
    act(C3, R1, AF.Identity, ["R1"], ["C3"], scale=1.0 / 16, bias=1.0)
    act(RM, R1, AF.Identity, ["R1"], ["RM"], scale=-15.0 / 16)
    act(J2, R1, AF.Identity, ["R1"], ["J2"], scale=2.0, bias=-2.0)
    act(T.co[:, 34:35], R1, AF.Identity, ["R1", "co"], ["cob7"], scale=2.0 ** -23 - 2.0 ** -20, bias=-2.0 ** -24)
    act(T.co[:, 42:43], R1, AF.Identity, ["R1", "co"], ["cob8"], scale=-2.0 ** -23, bias=2.0 ** -25)
    act(T.co[:, 2:32:8], T.co[:, 1:32:8], AF.Identity, ["RM", "coa3", "coa4", "coa5", "coa6"], ["cob"], scale=RM)
    act(NT1, T.t1[:, 15:16], AF.Identity, ["t1"], ["nt1"], scale=-1.0)
    act(T.w1[:, 0:1], P2, AF.Identity, ["t2", "w1"], ["w10"], scale=TAU)
    kcoa = ["coa%d" % k for k in range(3, 9)]
    kco = ["co", "cod", "cob", "cob7", "cob8", "coc"] + kcoa

    quant(T.uq[:], T.us[:], T.ut[:], ["ut"], ["uq"])
    cp(T.uq2[:].bitcast(dt.uint32), T.uq[:].bitcast(dt.uint32).indirect(T.uo[:]), ["uq", "uo"], ["uq2"])
    act(T.us2[:], T.us[:].indirect(T.uo[:]), AF.Copy, ["uq", "uo"], ["us2"])

    def equant(b):
        quant(T.eq[:, 128 * b:128 * b + 128], T.es[:, 128 * b:128 * b + 128], T.eb[:, 3 - b:515 - b], ["e+"], ["eq%d" % b])

    def clear(i):
        fill(T.sw[:, PL * i:PL * i + C], -256.0, ["sw%d" % i])

    def extras(k):
        if k == 0:
            ts(T.fh[:], T.f2[:], -0.5, 1.5, A.mult, A.add, ["f2"], ["fh"])
            op("v", lambda: V.reciprocal(KAP, C3), ["C3"], ["KAP"])
            scan(T.t3[:], T.fh[:], T.z16[:], C3, A.mult, A.add, ["fh", "z16", "C3"], ["K2"])
            fill(T.eb[:], 0.0, ["eb"])
        if k == -1:
            ts(T.w2[:, 0:2], T.w2[:, 0:2], 1.0, None, A.add, None, ["w2"], ["w2"])
            tt(T.co[:, 3:48:8], T.co[:, 2:48:8], T.co[:, 1:48:8], A.add, ["co", "cob", "cob7", "cob8"] + kcoa, ["coc"])
            ts(T.eb[:, 3:515:4], T.ai[:], 256.0, 64.0, A.is_equal, A.mult, ["ai", "eb"], ["e+"])
        if k == 3:
            equant(0)
            equant(1)
        if k == 6:
            equant(2)
        if k == 7:
            equant(3)
        if k == 8:
            ts(T.dmp[:], T.jm[:], R1, 2048.0, A.is_equal, A.mult, ["jm", "R1"], ["dmp"])
            clear(0)

    def extras_v(k):
        if k == 4:
            ts(T.mk0[:], T.jf[:, 0:32], float(C + 16), HH, A.is_ge, A.is_equal, ["jf", "HH"], ["mk0"])
        if k == 5:
            tt(T.tg[:], T.tg[:], T.mk0[:], A.mult, ["tg", "mk0"], ["tg"])

    def extras_a(k):
        if k == 1:
            act(JZ, R1, AF.Relu, ["R1"], ["JZ"], scale=-2.0, bias=4.0)
        if k == 2:
            act(NQ, HH, AF.Identity, ["HH", "R320"], ["NQ"], scale=16.0, bias=R320)
            act(I0, R1, AF.Identity, ["R1"], ["I0"], scale=-2.0 * FP, bias=2.0 * FP * 17 - F)
            act(JJ, R1, AF.Identity, ["R1"], ["JJ"], scale=2.0 * JW, bias=2.0 * (C - JW))
        if k == 3:
            act(NQ, NQ, AF.Identity, ["NQ"], ["NQ"], scale=-1.0, bias=-0.5)
            afill(T.ha[:, 0:4 * CP:4], CP, 0.0, [], ["ha0"])
            afill(T.ha[:, 1:4 * CP:4], CP, 1.0, [], ["ha1"])
        if k == 4:
            act(T.tg[:], T.jf[:, 0:32], AF.Sign, ["jf", "NQ"], ["tg"], bias=NQ)
            act(T.hb[:, UO:UO + 4 * CP:4], T.jf[:, 0:CP], AF.Identity, ["jf", "JJ"], ["hb0"], scale=2.0, bias=JJ)
            afill(T.hb[:, UO + 2:UO + 4 * CP:4], CP, 2.0 * PL, [], ["hb2"])
        if k == 5:
            afill(T.pl[:, 0:31], 31, 4096.0, [], ["pl0"])
            afill(T.pl[:, 31:33], 2, 0.0, [], ["pl1"])
            afill(T.fg[:, 65:66], 1, 0.0, [], ["fg0"])
        if k == 6:
            act(T.mb[:, 32:64], T.tg[:], AF.Identity, ["tg"], ["mb1"], scale=1024.0)
            afill(T.dq[:, 0:FP], FP, -BIG, [], ["dqa"])
            afill(T.dq[:, 3 * FP:4 * FP], FP, BIG, [], ["dqb"])
        if k == 7:
            act(T.mk0[:], T.tg[:], AF.Relu, ["tg"], ["mk0"], scale=-1.0)
        if k == 8:
            act(T.mb[:, 0:32], T.mk0[:], AF.Identity, ["mk0"], ["mb0"], scale=-1024.0)

    def th(k):
        return T.th[:, k:k + 1]

    def quant_state(t, i, src, reads):
        a, b = parts(TA[t])[i]
        quant(T["tq%d" % t][:, a:b], T["ts%d" % t][:, a:b], src[:, 4 * a:4 * b], reads, ["tq%d%d" % (t, i)])

    def scores(t, i):
        a, b = parts(TA[t])[i]
        for w in range(2):
            mx(2 * i + w, b - a, T.uq2[:, 128 * w:128 * w + 128], T.us2[:, 128 * w:128 * w + 128],
               T["tq%d" % t][:, a:b], T["ts%d" % t][:, a:b], ["uq2", "us2", "tq%d%d" % (t, i)])

    def relu_z(t, i):
        a, b = parts(TA[t])[i]
        if t == 0:
            act(T.xx[:, a:b], bank(2 * i, b - a), AF.Relu, ["bk%d" % (2 * i)], ["B%d" % i], scale=-1.0)
        else:
            act(T.nz[:, a:b], bank(2 * i, b - a), AF.Relu, ["bk%d" % (2 * i)], ["nz%d" % i], scale=-1.0)

    def abs_s(t, i):
        a, b = parts(TA[t])[i]
        act(T.ab[:, a:b], bank(2 * i + 1, b - a), AF.Abs, ["bk%d" % (2 * i + 1)], ["ab%d" % i])

    def low(t, i):
        a, b = parts(TA[t])[i]
        tt(T.xx[:, a:b], T.mm[:, a:b], T.nz[:, a:b], A.add, ["mm", "nz%d" % i], ["B%d" % i])

    def high(t, i):
        a, b = parts(TA[t])[i]
        tt(T.xx[:, C + a:C + b], T.xx[:, a:b], T.ab[:, a:b], A.add, ["B%d" % i, "ab%d" % i], ["HI%d" % i])

    def count1(a, b, col, reads, neg=False):
        if neg:
            act(T.junk[:, a:b], T.xx[:, a:b], AF.Sign, reads + ["nt1"], ["j%d" % col, "c%d" % col], bias=NT1, accum_out=T.sc[:, col:col + 1])
        else:
            act(T.junk[:, a:b], T.xx[:, a:b], AF.Sign, reads + ["t1"], ["j%d" % col, "c%d" % col], scale=-1.0, bias=T.t1[:, 15:16],
                accum_out=T.sc[:, col:col + 1])

    sent = 0
    KX = ["B0", "B1", "HI0", "HI1"]
    KJ = ["j9", "j10", "j11", "j12"]
    KR = ["r00", "r01", "r10", "r11"]
    quant_state(0, 0, T.xt, ["xt0"])
    scores(0, 0)
    quant_state(0, 1, T.xt, ["xt1"])
    scores(0, 1)
    op("y", lambda: Y.dma_start(T.wq[:].bitcast(dt.uint8), T.wc[:]), ["tq01"], ["wq"], sem="ldw", step=16, total=32)
    op("y", lambda: Y.dma_start(T.wp[:], T.ws[:]), [], ["wp"], sem="ldw", step=16, total=32)
    relu_z(0, 0)
    abs_s(0, 0)
    relu_z(0, 1)
    abs_s(0, 1)
    extras(0)
    high(0, 0)
    high(0, 1)
    extras(-1)

    for t in range(ROUNDS):
        other = T.cores[rank ^ PARTNER[t]]
        h1, h2, h3 = helpers(core, other, topo)
        tq, tsc, pq, psc = T["tq%d" % t], T["ts%d" % t], T["pq%d" % t], T["ps%d" % t]
        ao, la, sw = T["ao%d" % t], T["la%d" % t], T.sw
        ktq, kao, ksw = ["tq%d0" % t, "tq%d1" % t], "ao%d" % t, ["sw0", "sw1"]
        bulk, lst = T.sem["bulk%d" % t], T.sem["lst%d" % t]
        ta = TA[t]

        eng = topo.engines(core, h1)
        n = len(eng)
        trs = []
        for h, a, es in ((h1, 0, eng[:n // 2]), (h3, H, eng[n // 2:])):
            rid, pid = topo.addr(h, core)
            trs.append(RemoteDMATransfer(dst_ids=[DstId(rid=rid, pnc=pid)], dma_engine_mask=bits(es), remote_sem=bulk,
                                         src=tq[:, a:a + H].bitcast(dt.uint8), dst=pq[:, a:a + H].bitcast(dt.uint8)))
        rid2, pid2 = topo.addr(h2, core)
        op("g", lambda: g.remote_dma_fused(trs, local_sem=T.sem.sent), ktq, [], step=0)
        op("g", lambda: g.remote_dma(psc[:], tsc[:], bulk, T.sem.sent, pid2, rid2, bits(eng)), ktq, [], step=0)
        sent += 3 * n
        oh = helpers(other, core, topo)
        writer["pq"] = ("bulk%d" % t, sum(len(topo.engines(h, core)) for h in oh), {})
        readers["pq"] = []
        writer["la"] = ("lst%d" % t, len(topo.engines(oh[1], core)), {})
        readers["la"] = []

        count1(0, ta, 9, ["B0"])
        count1(C, C + ta, 11, ["HI0"])
        count1(ta, C, 10, ["B1"])
        count1(C + ta, F, 12, ["HI1"], neg=True)
        ts(T.sc[:, 13:14], T.sc[:, 10:11], T.sc[:, 11:12], T.sc[:, 9:10], A.add, A.add, ["c9", "c10", "c11"], ["c13"])
        for k in range(1, 9):
            off = T.of[:, 2 * k - 2:2 * k - 1]
            thr, kthr = th(k), "th%d" % k
            if k == 1:
                ts(off, T.sc[:, 12:13], T.sc[:, 13:14], J2, A.is_gt, A.add, ["c12", "c13", "J2"], ["of1"])
            else:
                d = SHARE[k]
                sk = T.sc[:, k:k + 1]
                src, ksrc = (T.xx, KX) if k < 7 else (T.dv, ["dv0", "dv1"])
                act(T.junk[:, d:F], src[:, d:F], AF.Sign, ksrc + [kthr], KJ + ["s%d" % k], scale=-1.0, bias=thr, accum_out=sk)
                if k == 2:
                    cp(T.pb[:, 0:1], thr, [kthr], ["pb0"])
                if k == 3:
                    ts(T.pb[:, 1:2], thr, KAP, None, A.mult, None, [kthr, "KAP"], ["pb1"])
                ts(T.gl[:, 0:d], src[:, 0:d], thr, None, A.is_gt, None, ksrc[:2] + [kthr], ["gl"])
                o = 8 * (k - 3)
                if k == 2:
                    ts(T.sc[:, 14:15], K2, T.pb[:, 0:1], None, A.mult, None, ["K2", "pb0"], ["sc2"])
                elif k == 3:
                    ts(T.dd[:], T.co[:], T.pb[:, 1:2], None, A.mult, None, kco + ["pb1"], ["ddu"] + ["dd%d" % j for j in range(3, 9)])
                elif k == 6:
                    ts(T.dd[:, o + 2:o + 4], T.dd[:, o + 2:o + 4], thr, th(4), A.add, A.subtract, ["dd6", kthr, "th4"], ["dd6"])
                else:
                    ts(T.dd[:, o + 2:o + 4], T.dd[:, o + 2:o + 4], thr, None, A.add, None, ["dd%d" % k, kthr], ["dd%d" % k])
                if t == 0:
                    extras_v(k)
                scan(T.mo[:, 0:d], T.gl[:, 0:d], T.gl[:, 0:d], float(-d), A.add, A.add, ["gl"], ["mo"])
                if k == 3:
                    ts(T.dd[:, 2:4], T.dd[:, 2:4], thr, None, A.add, None, ["dd3", kthr], ["dd3"])
                ts(off, T.mo[:, d - 1:d], sk, J2 if k == 2 else JZ, A.is_gt, A.add, ["mo", "s%d" % k, "J2", "JZ"], ["of%d" % k])
            if t == 0:
                extras_a(k)
            nxt, kn = th(k + 1), ["j16", "th%d" % (k + 1)]
            if k == 1:
                act(T.j16[:], T.w1[:].indirect(off), AF.Identity, ["w11", "w10", "of1"], kn, accum_out=nxt)
            elif k == 2:
                act(T.j16[:], T.w2[:].indirect(off), AF.Identity, ["w2", "of2", "sc2"], kn, scale=T.sc[:, 14:15], accum_out=nxt)
            else:
                act(T.j16[:], T.dd[:, o:o + 4].indirect(off), AF.Identity, ["dd%d" % k, "of%d" % k], kn, accum_out=nxt)
            if k in (1, 2):
                for i, (a, b) in enumerate(parts(ta)):
                    out, kb = T.rv[:, 2 * a + k - 1:2 * b:2], "bk%d" % (2 * i + 1)
                    if k == 1:
                        ts(out, bank(2 * i + 1, b - a), -1.0, 0.0, A.mult, A.max, [kb], ["r0%d" % i])
                    else:
                        ts(out, bank(2 * i + 1, b - a), 0.0, None, A.max, None, [kb], ["r1%d" % i])
            if k == 1:
                op("y", lambda: Y.dma_start(T.bd[:], T.xx[0:128:16, 0:C]), ["B0", "B1"], ["bd"], sem="deal", step=16, total=32 * (t + 1))
            if k == 2:
                op("y", lambda: Y.dma_start(T.rd[:], T.rv[0:128:16, :]), KR, ["rd"], sem="deal", step=16, total=32 * (t + 1))
                if t == 0:
                    op("y", lambda: Y.dma_start(T.vt[:], T.v[:]), ["rd"], ["vt"], sem="ldv", step=16)
            if k in (4, 5):
                a = C * (k - 4)
                ts(T.dv[:, a:a + C], T.xx[:, a:a + C], TAU, th(4), A.max, A.subtract, KX + ["th4"], ["dv%d" % (k - 4)])
            if k == 6:
                tt(T.cd[:, 0:FP:2], T.bd[:], T.rd[:, 0:FP:2], A.add, ["bd", "rd"], ["cd0"])
                tt(T.cd[:, 1:FP:2], T.bd[:], T.rd[:, 1:FP:2], A.add, ["bd", "rd"], ["cd1"])
            if k == 7:
                ts(T.dq[:, 2 * FP:3 * FP], T.cd[:], TAU, th(4), A.max, A.subtract, ["cd0", "cd1", "th4"], ["dq2"])
            if t == 0:
                extras(k)
            if k == 7:
                ts(T.dq[:, FP:2 * FP], T.dq[:, 2 * FP:3 * FP], T.dd[:, 44:45], None, A.subtract, None, ["dq2", "ddu"], ["dq1"])

        LO = th(9)
        act(T.jk2[:, 0:2 * FP], T.dq[:, 0:2 * FP], AF.Sign, ["dqa", "dq1", "th9"], ["jk0", "s0"], scale=-1.0, bias=LO, accum_out=T.sc[:, 0:1])
        act(T.jk2[:, 2 * FP:4 * FP], T.dq[:, 2 * FP:4 * FP], AF.Sign, ["dqb", "dq2", "th9"], ["jk1", "s1"], scale=-1.0, bias=LO, accum_out=T.sc[:, 1:2])
        ts(T.fg[:, 66:66 + 2 * FP], T.dq[:, FP:3 * FP], LO, 2.0, A.is_lt, A.mult, ["dq1", "dq2", "th9"], ["fgf"])
        lt = T.fg[:, 66 + FP:66 + 2 * FP]
        if t == 0:
            clear(1)
        scan(T.pl[:, 33:33 + FP], lt, lt, 0.0, A.add, A.max, ["fgf"], ["pl2"])
        ts(T.fl[:], T.mb[:], T.sc[:, 1:2], T.sc[:, 0:1], A.max, A.min, ["mb0", "mb1", "s0", "s1"], ["fl"])
        op("v", lambda: V.transpose(T.fg[:, 1:65], T.fl[:]), ["fl"], ["fgt"])
        scan(T.hb[:, 1:2 * (33 + FP):2], T.fg[:, 33:66 + FP], T.pl[:], I0, A.add, A.min, ["fgt", "fg0", "fgf", "I0", "pl0", "pl1", "pl2"], ["U"])
        op("v", lambda: V.tensor_reduce(T.sc[:, 15:16], T.fg[:, 0:33], AxisListType.X, A.add, negate=True), ["fgt", "I0"], ["L0"])
        u0, u1, u2 = (T.hb[:, UO + 3 + 2 * j:UO + 2 * j + 4 * CP:4] for j in range(3))
        tt(T.ha[:, 2:4 * CP:4], u2, u1, A.is_equal, ["U"], ["ha2"])
        tt(T.ha[:, 3:4 * CP:4], u1, u0, A.is_equal, ["U"], ["ha3"])
        scan(T.hs[:], T.ha[:], T.hb[:, UO:UO + 4 * CP], 0.0, A.mult, A.add, ["ha0", "ha1", "ha2", "ha3", "hb0", "hb2", "U"], ["hs"])
        ts(T.so[:], T.hs[:, 3:4 * CP:4], T.sc[:, 15:16], 0.5, A.add, A.mult, ["hs", "L0"], ["so"])
        cp(sw[:, 0:SW].indirect(T.so[:]), T.jv[:], ["so", "jv"], ksw)
        scan(T.fi[:], sw[:, 0:C], sw[:, PL:PL + C], -256.0, A.max, A.max, ksw, ["fi"])
        scan(T.gf[:], T.dmp[:], T.fi[:], 0.0, A.add, A.min, ["dmp", "fi"], ["gf"])
        ts(ao[:], T.gf[:, 15:C:16], float(H), None, A.add, None, ["gf"], [kao])
        op("g", lambda: g.remote_dma(la[:], ao[:], lst, T.sem.sent, pid2, rid2, bits(eng)), [kao], [], step=0)

        for b in range(4):
            unit(4 + b, b, tq, tsc, ktq)
        for b in range(4):
            unit(b, b, pq, psc, ["pq"])
        for b in range(4):
            act(T.dn[:, C * b:C * b + C], bank(4 + b), AF.Identity, ["bk%d" % (4 + b)], ["dn%d" % b], scale=1.0 / 64 if b % 2 else 1.0)
        for b in range(4):
            act(T.dp[:, C * b:C * b + C], bank(b), AF.Identity, ["bk%d" % b], ["dp%d" % b], scale=1.0 / 64)

        act(T.bg[:], T.xx[:, 0:C].indirect(ao[:]), AF.Copy, ["B0", "B1", kao], ["bg"])
        for b in (1, 3):
            act(T.hz[:, H * (b - 1):H * (b - 1) + C], T.dn[:, C * b:C * b + C].indirect(ao[:]), AF.Copy, ["dn%d" % b, kao], ["hz%d" % b])
        ts(T.bt[:], sw[:, 0:C], -256.0, 0.5, A.is_equal, A.mult, ksw, ["bt"])
        tt(T.kh[:], T.fi[:], T.bt[:], A.add, ["fi", "bt"], ["kh"])
        if t + 1 < ROUNDS:
            clear(0)
        scan(T.gk[:], T.dmp[:], T.kh[:], 0.0, A.add, A.min, ["dmp", "kh"], ["gk"])
        if t + 1 < ROUNDS:
            clear(1)
        if t == ROUNDS - 1:
            ts(T.kf[:], T.kh[:], 2.0, float(C), A.mult, A.add, ["kh"], ["kf"])
        ts(T.ko[:], T.gk[:, 15:C:16], 2.0, float(C), A.mult, A.add, ["gk"], ["ko"])
        if t == 1:
            quant(T.vq[:], T.vs[:], T.vt[:], ["vt"], ["vq"])
        tt(T.mm[:], T.rv[:].indirect(T.ko[:]), T.bg[:], A.add, KR + ["ko", "bg"], ["mm"])
        if t == ROUNDS - 1:
            op("y", lambda: Y.dma_start(T.kl[:], T.kf[0:128:16, :]), ["kf"], [], sem="stk", step=16)
            op("y", lambda: Y.dma_start(T.ml[:], T.mm[0:128:16, :]), ["mm"], [], sem="stk", step=16)

        def gather(e, b, i):
            lo, hi = parts(ZA)[i]
            out, win = T.zt[:, 4 * lo + b:4 * hi:4], T.dp[:, C * b:C * b + C].indirect(la[:, lo // 16:hi // 16])
            if e == "v":
                cp(out, win, ["dp%d" % b, "la"], ["zt%d%d" % (b, i)])
            else:
                act(out, win, AF.Copy, ["dp%d" % b, "la"], ["zt%d%d" % (b, i)])

        def products(i):
            lo, hi = parts(ZA)[i]
            quant(T.zq[:, lo:hi], T.zs[:, lo:hi], T.zt[:, 4 * lo:4 * hi], ["zt%d%d" % (b, i) for b in range(4)], ["zq%d" % i])
            for b in (1, 0, 3, 2):
                mx(2 * b + i, hi - lo, T.wq[:, 128 * b:128 * b + 128], T.wp[:, 128 * b:128 * b + 128], T.zq[:, lo:hi], T.zs[:, lo:hi],
                   ["wq", "wp", "zq%d" % i])

        def child(b, i):
            lo, hi = parts(ZA)[i]
            bk, kb, o = bank(2 * b + i, hi - lo), "bk%d" % (2 * b + i), F * (b // 2)
            for s in range(2):
                wr = ["ch%d%d%d" % (b, i, s)]
                if b % 2 == 0:
                    tt(T.tw[:, o + 2 * lo + s:o + 2 * hi:2], T.dn[:, C * b + lo:C * b + hi], bk, A.add if s == 0 else A.subtract, ["dn%d" % b, kb], wr)
                else:
                    act(T.rw[:, o + 2 * lo + s:o + 2 * hi:2], bk, AF.Identity, [kb], wr, scale=2.0 ** -6 if s == 0 else -2.0 ** -6)

        def pick(b, i):
            lo, hi = parts(TA[t + 1])[i]
            out, l, o = T.tt[:, 4 * lo + b:4 * hi:4], T.ko[:, lo // 16:hi // 16], F * (b // 2)
            rd, wr = ["ch%d%d%d" % (b, j, s) for j in range(2) for s in range(2)] + ["ko"], ["tt%d%d" % (b, i)]
            if b % 2 == 0:
                act(out, T.tw[:, o:o + F].indirect(l), AF.Identity, rd, wr, scale=2.0 ** -6)
            else:
                z = H * (b - 1)
                tt(out, T.rw[:, o:o + F].indirect(l), T.hz[:, z + lo:z + hi], A.add, rd + ["hz%d" % b], wr)

        for e, b, i in (("v", 0, 0), ("a", 2, 0), ("v", 1, 0), ("a", 3, 0), ("v", 0, 1), ("a", 2, 1), ("a", 3, 1)):
            gather(e, b, i)
        products(0)
        gather("v", 1, 1)
        products(1)
        for i in range(2):
            for b in (1, 0, 3, 2):
                child(b, i)
        for b in (1, 0, 3, 2):
            pick(b, 0)
        u = t + 1
        quant_state(u, 0, T.tt, ["tt%d0" % b for b in range(4)])
        for b in (1, 0, 3, 2):
            pick(b, 1)
        if u < ROUNDS:
            scores(u, 0)
            relu_z(u, 0)
            abs_s(u, 0)
            quant_state(u, 1, T.tt, ["tt%d1" % b for b in range(4)])
            scores(u, 1)
            relu_z(u, 1)
            abs_s(u, 1)
            low(u, 0)
            high(u, 0)
            low(u, 1)
            high(u, 1)

    tq, tsc = T["tq%d" % ROUNDS], T["ts%d" % ROUNDS]
    for i, (a, b) in enumerate(parts(TA[ROUNDS])):
        ktq = "tq%d%d" % (ROUNDS, i)
        if i == 1:
            quant_state(ROUNDS, 1, T.tt, ["tt%d1" % j for j in range(4)])
        mx(i, b - a, T.vq[:], T.vs[:], tq[:, a:b], tsc[:, a:b], ["vq", ktq])
        op("y", lambda: Y.dma_start(T.oc[:, 4 * a:4 * b], tq[:, a:b].bitcast(dt.uint8)), [ktq], [], sem="sto", step=16)
        if i == 0:
            act(T.yo[:, a:b], bank(i, b - a), AF.Copy, ["bk0"], ["yo0"])
            op("a", lambda: S.dma_start(T.y[:, a:b], T.yo[:, a:b]), ["yo0"], [], sem="sty", step=16)
        else:
            for k in range(4):
                op("y", lambda: Y.dma_start(T.osc[4 * k:4 * k + 4, :], tsc[32 * k:32 * k + 4, :]), [ktq], [], sem="sto", step=16)
            cp(T.yo[:, a:b], bank(i, b - a), ["bk1"], ["yo1"])
            op("a", lambda: S.dma_start(T.y[:, a:b], T.yo[:, a:b]), ["yo1"], [], sem="sty", step=16)
    g.wait_ge(T.sem.sent, sent)
    for s in ("sg", "sv", "sp", "sa", "stk", "sto", "sty", "deal"):
        g.wait_ge(T.sem[s], count[s])
